import numpy as np
import ml_dtypes


def mxq(x, axis, fmt="e4m3"):
    dtype, down = {"e4m3": (ml_dtypes.float8_e4m3fn, 7), "e5m2": (ml_dtypes.float8_e5m2, 14)}[fmt]
    v = np.moveaxis(np.asarray(x, np.float32).astype(ml_dtypes.bfloat16).astype(np.float64), axis, -1)
    blocks = v.reshape(v.shape[:-1] + (-1, 32))
    amax = np.abs(blocks).max(-1, keepdims=True)
    byte = np.maximum(np.where(amax > 0, np.frexp(amax)[1] - 1 + 127, 0) - down, 1)
    scale = np.exp2(byte - 127.0)
    codes = (blocks / scale).astype(np.float32).astype(dtype).astype(np.float64)
    return np.moveaxis((codes * scale).reshape(v.shape), -1, axis)


WIDE = False


def mx_kscale(k):
    if not WIDE:
        return np.ones(k)
    levels = np.array([10, -10, 5, -5, 0])
    if k % 512:
        return np.exp2(np.random.permutation(np.resize(levels, k // 32))).repeat(32)
    a = np.empty((k // 512, 16))
    for p in range(k // 512):
        a[p, :8] = np.random.permutation(np.resize(levels, 8))
        for g in range(8):
            far = levels[np.abs(levels - a[p, g]) >= 10]
            a[p, g + 8] = far[np.random.randint(len(far))]
    return np.exp2(a.ravel()).repeat(32)


def f64(x):
    return np.asarray(x).astype(np.float64)


def striped(idx):
    return np.tile(idx.reshape(-1, 16).T, (8, 1)).astype(np.uint16)


def unstriped(offs):
    return offs[:16].T.reshape(-1).astype(np.int64)


def pack_weight(w):
    k, n = w.shape
    w = f64(np.asarray(w, np.float32).astype(ml_dtypes.bfloat16)).reshape(k // 32, 32, n)
    amax = np.abs(w).max(1)
    byte = np.clip(np.where(amax > 0, np.frexp(amax)[1] - 1 + 127 - 7, 1), 1, 254)
    scaled = (w * np.exp2(127.0 - byte)[:, None, :]).reshape(k, n).astype(np.float32)
    words = np.ascontiguousarray(scaled.reshape(k // 512, 128, 4, n).transpose(0, 1, 3, 2)).astype(ml_dtypes.float8_e4m3fn).view(np.uint8)
    return words, np.ascontiguousarray(byte.astype(np.uint8).reshape(k // 512, 16, n))


def unpack_weight(words, scales):
    g, p, n, _ = words.shape
    vals = np.ascontiguousarray(words).view(ml_dtypes.float8_e4m3fn).astype(np.float64) * np.repeat(np.exp2(scales.astype(np.float64) - 127.0), 8, axis=1)[..., None]
    return vals.transpose(0, 1, 3, 2).reshape(g * 512, n)


E2M1 = np.array([0.0, 0.5, 1.0, 1.5, 2.0, 3.0, 4.0, 6.0, -0.0, -0.5, -1.0, -1.5, -2.0, -3.0, -4.0, -6.0])


def pack_fp4(w):
    k, n = w.shape
    w = f64(np.asarray(w, np.float32).astype(ml_dtypes.bfloat16)).reshape(k // 32, 32, n)
    amax = np.abs(w).max(1)
    mant, ex = np.frexp(amax / 6.0)
    byte = np.clip(np.where(amax > 0, np.where(mant > 0.5, ex, ex - 1) + 127, 1), 1, 254)
    scaled = (w * np.exp2(127.0 - byte)[:, None, :]).reshape(k, n).astype(np.float32)
    c = np.ascontiguousarray(scaled.reshape(k // 512, 128, 4, n).transpose(0, 1, 3, 2)).astype(ml_dtypes.float4_e2m1fn).view(np.uint8) & 0xF
    words = (c[..., 0::2] | (c[..., 1::2] << 4)).reshape(k // 512, 128, 2 * n)
    return np.ascontiguousarray(words), np.ascontiguousarray(byte.astype(np.uint8).reshape(k // 512, 16, n))


def unpack_fp4(words, scales):
    g, _, n = scales.shape
    words = np.ascontiguousarray(words).reshape(g, 128, n, 2)
    nib = np.empty((g, 128, n, 4), np.uint8)
    nib[..., 0::2] = words & 0xF
    nib[..., 1::2] = words >> 4
    vals = E2M1[nib] * np.repeat(np.exp2(scales.astype(np.float64) - 127.0), 8, axis=1)[..., None]
    return vals.transpose(0, 1, 3, 2).reshape(g * 512, n)


def relu(v):
    return np.maximum(v, 0.0)


K, T, S, H, N, U, V = 512, 2048, 1024, 512, 128, 1024, 512


def setup_inputs():
    n = np.random.standard_normal
    s = mx_kscale(K)[:, None]
    u = mx_kscale(H)
    packed_xT = pack_weight(n((K, T)) * s)
    packed_w3 = pack_fp4(n((H, N)) / np.sqrt(H) / u[:, None])
    return {
        "x_words": packed_xT[0],
        "x_scales": packed_xT[1],
        "w1": (n((K, H)) / np.sqrt(K) / s * u).astype(np.float32),
        "w2": (n((K, H)) / np.sqrt(K) / s * u).astype(np.float32),
        "w3_words": packed_w3[0],
        "w3_scales": packed_w3[1],
        "offs": striped(np.random.permutation(T)[:S]),
        "near": striped(np.random.permutation(U)[:V]),
        "far": striped(np.random.permutation(U)[:V]),
    }


def reference(x_words, x_scales, w1, w2, w3_words, w3_scales, offs, near, far):
    xq = unpack_weight(x_words, x_scales)[:, unstriped(offs)]
    a = np.zeros((H, S))
    a[:, unstriped(near)] = relu(mxq(f64(w1), 0, "e4m3").T @ xq[:, :V])
    e = np.zeros((H, S))
    e[:, unstriped(far)] = relu(mxq(f64(w2), 0, "e4m3").T @ xq[:, V:2 * V])
    z = np.maximum(a, e)
    return unpack_fp4(w3_words, w3_scales).T @ mxq(z, 0, "e4m3")

@@ -1,0 +1,160 @@
+from contextlib import ExitStack
+
+import concourse.mybir as mybir
+
+K, T, S, H, N, V = 512, 2048, 1024, 512, 128, 512
+FLOPS = 2 * K * H * V * 2 + 2 * H * N * S
+
+F32 = mybir.dt.float32
+BF16 = mybir.dt.bfloat16
+I32 = mybir.dt.int32
+U32 = mybir.dt.uint32
+U16 = mybir.dt.uint16
+U8 = mybir.dt.uint8
+FP8X4 = mybir.dt.float8_e4m3fn_x4
+FP4X4 = mybir.dt.float4_e2m1fn_x4
+RELU = mybir.ActivationFunctionType.Relu
+MAX = mybir.AluOpType.max
+SUB = mybir.AluOpType.subtract
+ADD = mybir.AluOpType.add
+
+P = 128
+PACK = 4
+
+
+def tile_picked_bev_max_p_kernel(
+    tc, x_words, x_scales, w1, w2, w3_words, w3_scales, offs, near, far, out
+):
+    nc = tc.nc
+    with ExitStack() as ctx:
+        keep = ctx.enter_context(tc.tile_pool(name="keep", bufs=1))
+        psum = ctx.enter_context(tc.psum_pool(name="psum", bufs=4))
+
+        offs_t = keep.tile([P, S // 16], U16, name="offs_t")
+        near_t = keep.tile([P, V // 16], U16, name="near_t")
+        far_t = keep.tile([P, V // 16], U16, name="far_t")
+        xw = keep.tile([P, T], I32, name="xw", align_bytes=64)
+        xs = keep.tile([P, T], U8, name="xs", align_bytes=64)
+        w3w = keep.tile([P, 2 * N], U8, name="w3w", align_bytes=64)
+        w3s = keep.tile([P, N], U8, name="w3s", align_bytes=64)
+
+        nc.vector.memset(xs[:].bitcast(I32), 0)
+        nc.sync.dma_start(offs_t[:], offs)
+        nc.sync.dma_start(near_t[:], near)
+        nc.sync.dma_start(far_t[:], far)
+        for q in range(4):
+            nc.sync.dma_start(out=xs[32 * q : 32 * q + 4, :].bitcast(I32), in_=x_scales[0, 4 * q : 4 * q + 4, :].bitcast(I32))
+        w1_raw = keep.tile([P, PACK, H], F32, name="w1_raw")
+        nc.sync.dma_start(out=w1_raw[:], in_=w1.rearrange("(p j) c -> p j c", j=PACK))
+        nc.sync.dma_start(out=xw[:], in_=x_words[0].rearrange("p n t -> p (n t)").bitcast(I32))
+        w2_raw = keep.tile([P, PACK, H], F32, name="w2_raw", tag="w2_raw")
+        nc.sync.dma_start(out=w2_raw[:], in_=w2.rearrange("(p j) c -> p j c", j=PACK))
+        nc.vector.memset(w3s[:].bitcast(I32), 0)
+        nc.sync.dma_start(out=w3w[:].bitcast(I32), in_=w3_words[0].bitcast(I32))
+        for q in range(4):
+            nc.sync.dma_start(out=w3s[32 * q : 32 * q + 4, :].bitcast(I32), in_=w3_scales[0, 4 * q : 4 * q + 4, :].bitcast(I32))
+
+        wins = [[keep.tile([P, S], F32, name=f"win{s}_{b}") for b in range(2)] for s in range(2)]
+        for s in range(2):
+            for b in range(2):
+                nc.vector.memset(wins[s][b][:], 0.0)
+
+        gw = [keep.tile([P, V], U32, name=f"gw{s}", align_bytes=64) for s in range(2)]
+        gs = [keep.tile([P, V], U8, name=f"gs{s}", align_bytes=64) for s in range(2)]
+        for s in range(2):
+            nc.vector.tensor_copy(out=gs[s][:], in_=xs[:].indirect(offs_t[:, s * (V // 16) : (s + 1) * (V // 16)]))
+
+        def cast(copy, grouped, raw, m0, m1):
+            copy(
+                out=grouped[:].rearrange("p (t m j) -> p m j t", t=PACK, j=PACK)[:, m0:m1],
+                in_=raw[:].rearrange("p j (m t) -> p m j t", t=PACK)[:, m0:m1],
+            )
+
+        def quant(grouped, t0, t1, name):
+            n = (t1 - t0) * P
+            codes = keep.tile([P, n], U32, name=name + "c", align_bytes=64)
+            scales = keep.tile([P, n], U8, name=name + "s", align_bytes=64)
+            nc.vector.quantize_mx(out=codes[:].bitcast(FP8X4), scales=scales[:], in_=grouped[:, t0 * PACK * P : t1 * PACK * P])
+            return [(codes[:, (t - t0) * P : (t - t0 + 1) * P], scales[:, (t - t0) * P : (t - t0 + 1) * P]) for t in range(t0, t1)]
+
+        def layer(s, wq, src, v0=0, v1=V):
+            acc = psum.tile([P, V], F32, name="acc")
+            nc.tensor.matmul_mx(out=acc[:, : v1 - v0], lhsT=wq[0].bitcast(FP8X4), lhsT_scale=wq[1], rhs=gw[s][:, v0:v1].bitcast(FP8X4), rhs_scale=gs[s][:, v0:v1], start=True, stop=True)
+            nc.scalar.activation(out=src[:, v0:v1], in_=acc[:, : v1 - v0], func=RELU)
+
+        lists = [near_t, far_t]
+
+        def scatter(s, t, src, v0=0, v1=V):
+            nc.vector.tensor_copy(out=wins[s][t % 2][:].indirect(lists[s][:, v0 // 16 : v1 // 16]), in_=src[:, v0:v1])
+
+        g1 = keep.tile([P, PACK * H], BF16, name="g1", tag="grouped", align_bytes=64)
+        cast(nc.scalar.copy, g1, w1_raw, 0, 64)
+        cast(nc.vector.tensor_copy, g1, w1_raw, 64, 128)
+        wq1 = quant(g1, 0, 4, "qa")
+
+        for v0, v1 in ((0, 256), (256, 512), (512, 1024)):
+            nc.vector.tensor_copy(out=gw[v0 // V][:, v0 % V : v0 % V + v1 - v0], in_=xw[:].bitcast(U32).indirect(offs_t[:, v0 // 16 : v1 // 16]))
+
+        src = keep.tile([P, V], F32, name="src0_0")
+        for v0 in (0, 256):
+            layer(0, wq1[0], src, v0, v0 + 256)
+        for v0 in (0, 256):
+            scatter(0, 0, src, v0, v0 + 256)
+
+        g2 = keep.tile([P, PACK * H], BF16, name="g2", tag="grouped", align_bytes=64)
+        for h in range(4):
+            cast(nc.scalar.copy, g2, w2_raw, 32 * h, 32 * (h + 1))
+        wq2 = quant(g2, 0, 4, "qe")
+        wq = [wq1, wq2]
+
+        zp = [keep.tile([P, 2, S], BF16, name=f"zp{u}") for u in range(2)]
+        chunks = [slice(0, 256), slice(256, 512), slice(512, 768), slice(768, 896), slice(896, 1024)]
+        nch = len(chunks)
+        zin = [keep.tile([P, chunks[c].stop - chunks[c].start, PACK], BF16, name=f"zin{c}", align_bytes=64) for c in range(nch)]
+
+        def join(t, cols):
+            nc.vector.tensor_tensor(out=zp[t // 2][:, t % 2, cols], in0=wins[0][t % 2][:, cols], in1=wins[1][t % 2][:, cols], op=MAX)
+
+        def join_aside(t):
+            halves = [slice(h * (S // 2), (h + 1) * (S // 2)) for h in range(2)]
+            diff = [keep.tile([P, S // 2], F32, name=f"diff{h}") for h in range(2)]
+            for h in range(2):
+                nc.gpsimd.tensor_tensor(out=diff[h][:], in0=wins[0][t % 2][:, halves[h]], in1=wins[1][t % 2][:, halves[h]], op=SUB)
+                nc.scalar.activation(out=diff[h][:], in_=diff[h][:], func=RELU)
+            for h in range(2):
+                nc.gpsimd.tensor_tensor(out=zp[t // 2][:, t % 2, halves[h]], in0=diff[h][:], in1=wins[1][t % 2][:, halves[h]], op=ADD)
+
+        def weave(u, c, copy):
+            copy(out=zin[c][:, :, 2 * u : 2 * u + 2], in_=zp[u][:, :, chunks[c]].rearrange("p t c -> p c t"))
+
+        src = keep.tile([P, V], F32, name="src_a1", tag="w2_raw")
+        layer(0, wq1[1], src)
+        scatter(0, 1, src)
+        for s, t in ((1, 0), (1, 1), (0, 2), (1, 2), (0, 3), (1, 3)):
+            src = keep.tile([P, V], F32, name=f"src{s}_{t}")
+            layer(s, wq[s][t], src)
+            scatter(s, t, src)
+            if s == 1 and t < 3:
+                join_aside(t)
+            if s == 1 and t == 1:
+                for c in range(nch):
+                    weave(0, c, nc.scalar.copy)
+
+        for h in range(4):
+            join(3, slice(h * 256, (h + 1) * 256))
+        for c in range(nch):
+            weave(1, c, nc.scalar.copy if c < 2 else nc.vector.tensor_copy)
+        for c in range(nch):
+            cols = chunks[c]
+            n = cols.stop - cols.start
+            zc = keep.tile([P, n], U32, name=f"zc{c}", align_bytes=64)
+            zs = keep.tile([P, n], U8, name=f"zs{c}", align_bytes=64)
+            nc.vector.quantize_mx(out=zc[:].bitcast(FP8X4), scales=zs[:], in_=zin[c][:].rearrange("p c t -> p (c t)"))
+            acc = psum.tile([P, V], F32, name="acc")
+            nc.tensor.matmul_mx(out=acc[:, :n], lhsT=w3w[:].bitcast(FP4X4), lhsT_scale=w3s[:], rhs=zc[:].bitcast(FP8X4), rhs_scale=zs[:], start=True, stop=True)
+            res = keep.tile([P, n], F32, name=f"res{c}")
+            if c == nch - 1:
+                nc.vector.tensor_copy(out=res[:], in_=acc[:, :n])
+            else:
+                nc.scalar.copy(out=res[:], in_=acc[:, :n])
+            nc.sync.dma_start(out=out[:, cols], in_=res[:])

@@ -38,7 +38,7 @@ def tile_picked_bev_max_p_kernel(
         w3w = keep.tile([P, 2 * N], U8, name="w3w", align_bytes=64)
         w3s = keep.tile([P, N], U8, name="w3s", align_bytes=64)
 
-        nc.vector.memset(xs[:].bitcast(I32), 0)
+        nc.gpsimd.memset(xs[:].bitcast(I32), 0)
         nc.sync.dma_start(offs_t[:], offs)
         nc.sync.dma_start(near_t[:], near)
         nc.sync.dma_start(far_t[:], far)
@@ -49,7 +49,7 @@ def tile_picked_bev_max_p_kernel(
         nc.sync.dma_start(out=xw[:], in_=x_words[0].rearrange("p n t -> p (n t)").bitcast(I32))
         w2_raw = keep.tile([P, PACK, H], F32, name="w2_raw", tag="w2_raw")
         nc.sync.dma_start(out=w2_raw[:], in_=w2.rearrange("(p j) c -> p j c", j=PACK))
-        nc.vector.memset(w3s[:].bitcast(I32), 0)
+        nc.gpsimd.memset(w3s[:].bitcast(I32), 0)
         nc.sync.dma_start(out=w3w[:].bitcast(I32), in_=w3_words[0].bitcast(I32))
         for q in range(4):
             nc.sync.dma_start(out=w3s[32 * q : 32 * q + 4, :].bitcast(I32), in_=w3_scales[0, 4 * q : 4 * q + 4, :].bitcast(I32))
@@ -57,9 +57,8 @@ def tile_picked_bev_max_p_kernel(
         wins = [[keep.tile([P, S], F32, name=f"win{s}_{b}") for b in range(2)] for s in range(2)]
         for s in range(2):
             for b in range(2):
-                nc.vector.memset(wins[s][b][:], 0.0)
+                nc.gpsimd.memset(wins[s][b][:], 0.0)
 
-        gw = [keep.tile([P, V], U32, name=f"gw{s}", align_bytes=64) for s in range(2)]
         gs = [keep.tile([P, V], U8, name=f"gs{s}", align_bytes=64) for s in range(2)]
         for s in range(2):
             nc.vector.tensor_copy(out=gs[s][:], in_=xs[:].indirect(offs_t[:, s * (V // 16) : (s + 1) * (V // 16)]))
@@ -77,31 +76,39 @@ def tile_picked_bev_max_p_kernel(
             nc.vector.quantize_mx(out=codes[:].bitcast(FP8X4), scales=scales[:], in_=grouped[:, t0 * PACK * P : t1 * PACK * P])
             return [(codes[:, (t - t0) * P : (t - t0 + 1) * P], scales[:, (t - t0) * P : (t - t0 + 1) * P]) for t in range(t0, t1)]
 
-        def layer(s, wq, src, v0=0, v1=V):
+        def product(s, wq, v0, v1):
             acc = psum.tile([P, V], F32, name="acc")
-            nc.tensor.matmul_mx(out=acc[:, : v1 - v0], lhsT=wq[0].bitcast(FP8X4), lhsT_scale=wq[1], rhs=gw[s][:, v0:v1].bitcast(FP8X4), rhs_scale=gs[s][:, v0:v1], start=True, stop=True)
-            nc.scalar.activation(out=src[:, v0:v1], in_=acc[:, : v1 - v0], func=RELU)
+            nc.tensor.matmul_mx(out=acc[:, : v1 - v0], lhsT=wq[0].bitcast(FP8X4), lhsT_scale=wq[1], rhs=gw[:, s * V + v0 : s * V + v1].bitcast(FP8X4), rhs_scale=gs[s][:, v0:v1], start=True, stop=True)
+            return acc
+
+        def layer(s, wq, src, v0, v1):
+            acc = product(s, wq, v0, v1)
+            nc.scalar.activation(out=src, in_=acc[:, : v1 - v0], func=RELU)
 
         lists = [near_t, far_t]
 
         def scatter(s, t, src, v0=0, v1=V):
-            nc.vector.tensor_copy(out=wins[s][t % 2][:].indirect(lists[s][:, v0 // 16 : v1 // 16]), in_=src[:, v0:v1])
+            nc.vector.tensor_copy(out=wins[s][t % 2][:].indirect(lists[s][:, v0 // 16 : v1 // 16]), in_=src)
 
         g1 = keep.tile([P, PACK * H], BF16, name="g1", tag="grouped", align_bytes=64)
         cast(nc.scalar.copy, g1, w1_raw, 0, 64)
         cast(nc.vector.tensor_copy, g1, w1_raw, 64, 128)
         wq1 = quant(g1, 0, 4, "qa")
 
+        gw = keep.tile([P, S], U32, name="gw", tag="grouped", align_bytes=64)
         for v0, v1 in ((0, 256), (256, 512), (512, 1024)):
-            nc.vector.tensor_copy(out=gw[v0 // V][:, v0 % V : v0 % V + v1 - v0], in_=xw[:].bitcast(U32).indirect(offs_t[:, v0 // 16 : v1 // 16]))
+            nc.vector.tensor_copy(out=gw[:, v0:v1], in_=xw[:].bitcast(U32).indirect(offs_t[:, v0 // 16 : v1 // 16]))
 
-        src = keep.tile([P, V], F32, name="src0_0")
-        for v0 in (0, 256):
-            layer(0, wq1[0], src, v0, v0 + 256)
-        for v0 in (0, 256):
-            scatter(0, 0, src, v0, v0 + 256)
+        first = keep.tile([P, 128], F32, name="first", tag="first", align_bytes=64)
+        rest = keep.tile([P, V - 128], F32, name="rest")
+        acc = product(0, wq1[0], 0, 256)
+        nc.scalar.activation(out=first[:], in_=acc[:, :128], func=RELU)
+        nc.scalar.activation(out=rest[:, :128], in_=acc[:, 128:256], func=RELU)
+        layer(0, wq1[0], rest[:, 128:], 256, V)
+        scatter(0, 0, first[:], 0, 128)
+        scatter(0, 0, rest[:], 128, V)
 
-        g2 = keep.tile([P, PACK * H], BF16, name="g2", tag="grouped", align_bytes=64)
+        g2 = keep.tile([P, PACK * H], BF16, name="g2", tag="first", align_bytes=64)
         for h in range(4):
             cast(nc.scalar.copy, g2, w2_raw, 32 * h, 32 * (h + 1))
         wq2 = quant(g2, 0, 4, "qe")
@@ -127,16 +134,16 @@ def tile_picked_bev_max_p_kernel(
         def weave(u, c, copy):
             copy(out=zin[c][:, :, 2 * u : 2 * u + 2], in_=zp[u][:, :, chunks[c]].rearrange("p t c -> p c t"))
 
-        src = keep.tile([P, V], F32, name="src_a1", tag="w2_raw")
-        layer(0, wq1[1], src)
-        scatter(0, 1, src)
-        for s, t in ((1, 0), (1, 1), (0, 2), (1, 2), (0, 3), (1, 3)):
-            src = keep.tile([P, V], F32, name=f"src{s}_{t}")
-            layer(s, wq[s][t], src)
-            scatter(s, t, src)
-            if s == 1 and t < 3:
+        src = keep.tile([P, 256], F32, name="src_a1", tag="w2_raw")
+        layer(0, wq1[1], src[:], 0, 256)
+        scatter(0, 1, src[:], 0, 256)
+        for s, t, v0, tag in ((1, 0, 0, "e0"), (1, 1, 0, "e1"), (0, 1, 256, "e0"), (0, 2, 0, "a2"), (1, 2, 0, "e2"), (0, 3, 0, "a3"), (1, 3, 0, "e3")):
+            src = keep.tile([P, V - v0], F32, name=f"src{s}_{t}", tag=tag)
+            layer(s, wq[s][t], src[:], v0, V)
+            scatter(s, t, src[:], v0, V)
+            if (s, t) in ((1, 0), (0, 1), (1, 2)):
                 join_aside(t)
-            if s == 1 and t == 1:
+            if (s, t) == (0, 1):
                 for c in range(nch):
                     weave(0, c, nc.scalar.copy)
 

@@ -57,7 +57,7 @@ def tile_picked_bev_max_p_kernel(
         wins = [[keep.tile([P, S], F32, name=f"win{s}_{b}") for b in range(2)] for s in range(2)]
         for s in range(2):
             for b in range(2):
-                nc.gpsimd.memset(wins[s][b][:], 0.0)
+                nc.vector.memset(wins[s][b][:], 0.0)
 
         gs = [keep.tile([P, V], U8, name=f"gs{s}", align_bytes=64) for s in range(2)]
         for s in range(2):
@@ -71,19 +71,15 @@ def tile_picked_bev_max_p_kernel(
 
         def quant(grouped, t0, t1, name):
             n = (t1 - t0) * P
-            codes = keep.tile([P, n], U32, name=name + "c", align_bytes=64)
+            codes = keep.tile([P, n], U32, name=name + "c", tag=name, align_bytes=64)
             scales = keep.tile([P, n], U8, name=name + "s", align_bytes=64)
             nc.vector.quantize_mx(out=codes[:].bitcast(FP8X4), scales=scales[:], in_=grouped[:, t0 * PACK * P : t1 * PACK * P])
             return [(codes[:, (t - t0) * P : (t - t0 + 1) * P], scales[:, (t - t0) * P : (t - t0 + 1) * P]) for t in range(t0, t1)]
 
-        def product(s, wq, v0, v1):
-            acc = psum.tile([P, V], F32, name="acc")
+        def product(s, wq, v0, v1, tag="acc"):
+            acc = psum.tile([P, V], F32, name=tag, tag=tag)
             nc.tensor.matmul_mx(out=acc[:, : v1 - v0], lhsT=wq[0].bitcast(FP8X4), lhsT_scale=wq[1], rhs=gw[:, s * V + v0 : s * V + v1].bitcast(FP8X4), rhs_scale=gs[s][:, v0:v1], start=True, stop=True)
             return acc
-
-        def layer(s, wq, src, v0, v1):
-            acc = product(s, wq, v0, v1)
-            nc.scalar.activation(out=src, in_=acc[:, : v1 - v0], func=RELU)
 
         lists = [near_t, far_t]
 
@@ -93,22 +89,26 @@ def tile_picked_bev_max_p_kernel(
         g1 = keep.tile([P, PACK * H], BF16, name="g1", tag="grouped", align_bytes=64)
         cast(nc.scalar.copy, g1, w1_raw, 0, 64)
         cast(nc.vector.tensor_copy, g1, w1_raw, 64, 128)
-        wq1 = quant(g1, 0, 4, "qa")
+        wq1 = quant(g1, 0, 1, "qa0") + quant(g1, 1, 2, "qa1") + quant(g1, 2, 4, "qa2")
 
         gw = keep.tile([P, S], U32, name="gw", tag="grouped", align_bytes=64)
         for v0, v1 in ((0, 256), (256, 512), (512, 1024)):
             nc.vector.tensor_copy(out=gw[:, v0:v1], in_=xw[:].bitcast(U32).indirect(offs_t[:, v0 // 16 : v1 // 16]))
 
-        first = keep.tile([P, 128], F32, name="first", tag="first", align_bytes=64)
-        rest = keep.tile([P, V - 128], F32, name="rest")
-        acc = product(0, wq1[0], 0, 256)
-        nc.scalar.activation(out=first[:], in_=acc[:, :128], func=RELU)
-        nc.scalar.activation(out=rest[:, :128], in_=acc[:, 128:256], func=RELU)
-        layer(0, wq1[0], rest[:, 128:], 256, V)
-        scatter(0, 0, first[:], 0, 128)
-        scatter(0, 0, rest[:], 128, V)
+        def relu_out(acc, v0, v1, tag):
+            src = keep.tile([P, v1 - v0], F32, name="src_" + tag, tag=tag)
+            nc.scalar.activation(out=src[:], in_=acc, func=RELU)
+            return src[:]
 
-        g2 = keep.tile([P, PACK * H], BF16, name="g2", tag="first", align_bytes=64)
+        acc = product(0, wq1[0], 0, 256)
+        scatter(0, 0, relu_out(acc[:, :256], 0, 256, "a0a"), 0, 256)
+        acc1 = product(0, wq1[1], 0, V, "held")
+        acc = product(0, wq1[0], 256, V)
+        late = relu_out(acc[:, :256], 256, V, "a0b")
+        scatter(0, 1, relu_out(acc1[:, :128], 0, 128, "a1a"), 0, 128)
+        scatter(0, 0, late, 256, V)
+
+        g2 = keep.tile([P, PACK * H], BF16, name="g2", tag="qa0", align_bytes=64)
         for h in range(4):
             cast(nc.scalar.copy, g2, w2_raw, 32 * h, 32 * (h + 1))
         wq2 = quant(g2, 0, 4, "qe")
@@ -134,18 +134,18 @@ def tile_picked_bev_max_p_kernel(
         def weave(u, c, copy):
             copy(out=zin[c][:, :, 2 * u : 2 * u + 2], in_=zp[u][:, :, chunks[c]].rearrange("p t c -> p c t"))
 
-        src = keep.tile([P, 256], F32, name="src_a1", tag="w2_raw")
-        layer(0, wq1[1], src[:], 0, 256)
-        scatter(0, 1, src[:], 0, 256)
-        for s, t, v0, tag in ((1, 0, 0, "e0"), (1, 1, 0, "e1"), (0, 1, 256, "e0"), (0, 2, 0, "a2"), (1, 2, 0, "e2"), (0, 3, 0, "a3"), (1, 3, 0, "e3")):
-            src = keep.tile([P, V - v0], F32, name=f"src{s}_{t}", tag=tag)
-            layer(s, wq[s][t], src[:], v0, V)
-            scatter(s, t, src[:], v0, V)
-            if (s, t) in ((1, 0), (0, 1), (1, 2)):
-                join_aside(t)
-            if (s, t) == (0, 1):
-                for c in range(nch):
-                    weave(0, c, nc.scalar.copy)
+        scatter(0, 1, relu_out(acc1[:, 128:384], 128, 384, "w2_raw"), 128, 384)
+        for s, t in ((1, 0), (1, 1), (0, 2), (1, 2), (0, 3), (1, 3)):
+            acc = product(s, wq[s][t], 0, V)
+            scatter(s, t, relu_out(acc[:], 0, V, f"s{s}{t}"), 0, V)
+            if (s, t) == (1, 1):
+                scatter(0, 1, relu_out(acc1[:, 384:], 384, V, "s10"), 384, V)
+            if s == 1:
+                if t < 3:
+                    join_aside(t)
+                if t == 1:
+                    for c in range(nch):
+                        weave(0, c, nc.scalar.copy)
 
         for h in range(4):
             join(3, slice(h * 256, (h + 1) * 256))

@@ -55,9 +55,9 @@ def tile_picked_bev_max_p_kernel(
             nc.sync.dma_start(out=w3s[32 * q : 32 * q + 4, :].bitcast(I32), in_=w3_scales[0, 4 * q : 4 * q + 4, :].bitcast(I32))
 
         wins = [[keep.tile([P, S], F32, name=f"win{s}_{b}") for b in range(2)] for s in range(2)]
-        for s in range(2):
-            for b in range(2):
-                nc.vector.memset(wins[s][b][:], 0.0)
+        for b in range(2):
+            nc.vector.memset(wins[0][b][:], 0.0)
+            nc.scalar.copy(out=wins[1][b][:], in_=wins[0][b][:])
 
         gs = [keep.tile([P, V], U8, name=f"gs{s}", align_bytes=64) for s in range(2)]
         for s in range(2):
@@ -65,8 +65,8 @@ def tile_picked_bev_max_p_kernel(
 
         def cast(copy, grouped, raw, m0, m1):
             copy(
-                out=grouped[:].rearrange("p (t m j) -> p m j t", t=PACK, j=PACK)[:, m0:m1],
-                in_=raw[:].rearrange("p j (m t) -> p m j t", t=PACK)[:, m0:m1],
+                out=grouped[:].rearrange("p (t m j) -> p m t j", t=PACK, j=PACK)[:, m0:m1],
+                in_=raw[:].rearrange("p j (m t) -> p m t j", t=PACK)[:, m0:m1],
             )
 
         def quant(grouped, t0, t1, name):
@@ -87,8 +87,8 @@ def tile_picked_bev_max_p_kernel(
             nc.vector.tensor_copy(out=wins[s][t % 2][:].indirect(lists[s][:, v0 // 16 : v1 // 16]), in_=src)
 
         g1 = keep.tile([P, PACK * H], BF16, name="g1", tag="grouped", align_bytes=64)
-        cast(nc.scalar.copy, g1, w1_raw, 0, 64)
-        cast(nc.vector.tensor_copy, g1, w1_raw, 64, 128)
+        cast(nc.scalar.copy, g1, w1_raw, 0, 56)
+        cast(nc.vector.tensor_copy, g1, w1_raw, 56, 128)
         wq1 = quant(g1, 0, 1, "qa0") + quant(g1, 1, 2, "qa1") + quant(g1, 2, 4, "qa2")
 
         gw = keep.tile([P, S], U32, name="gw", tag="grouped", align_bytes=64)
@@ -114,25 +114,23 @@ def tile_picked_bev_max_p_kernel(
         wq2 = quant(g2, 0, 4, "qe")
         wq = [wq1, wq2]
 
-        zp = [keep.tile([P, 2, S], BF16, name=f"zp{u}") for u in range(2)]
-        chunks = [slice(0, 256), slice(256, 512), slice(512, 768), slice(768, 896), slice(896, 1024)]
+        groups = [slice(0, 512), slice(512, 1024)]
+        chunks = [(0, 0, 256), (0, 256, 512), (1, 0, 128), (1, 128, 384), (1, 384, 512)]
         nch = len(chunks)
-        zin = [keep.tile([P, chunks[c].stop - chunks[c].start, PACK], BF16, name=f"zin{c}", align_bytes=64) for c in range(nch)]
-
-        def join(t, cols):
-            nc.vector.tensor_tensor(out=zp[t // 2][:, t % 2, cols], in0=wins[0][t % 2][:, cols], in1=wins[1][t % 2][:, cols], op=MAX)
+        zp = [[keep.tile([P, 2, g.stop - g.start], BF16, name=f"zp{u}_{g.start}") for g in groups] for u in range(2)]
+        zin = [keep.tile([P, c1 - c0, PACK], BF16, name=f"zin{c}", align_bytes=64) for c, (g, c0, c1) in enumerate(chunks)]
 
         def join_aside(t):
-            halves = [slice(h * (S // 2), (h + 1) * (S // 2)) for h in range(2)]
-            diff = [keep.tile([P, S // 2], F32, name=f"diff{h}") for h in range(2)]
-            for h in range(2):
-                nc.gpsimd.tensor_tensor(out=diff[h][:], in0=wins[0][t % 2][:, halves[h]], in1=wins[1][t % 2][:, halves[h]], op=SUB)
-                nc.scalar.activation(out=diff[h][:], in_=diff[h][:], func=RELU)
-            for h in range(2):
-                nc.gpsimd.tensor_tensor(out=zp[t // 2][:, t % 2, halves[h]], in0=diff[h][:], in1=wins[1][t % 2][:, halves[h]], op=ADD)
+            diff = [keep.tile([P, g.stop - g.start], F32, name=f"diff{g.start}") for g in groups]
+            for i, g in enumerate(groups):
+                nc.gpsimd.tensor_tensor(out=diff[i][:], in0=wins[0][t % 2][:, g], in1=wins[1][t % 2][:, g], op=SUB)
+                nc.scalar.activation(out=diff[i][:], in_=diff[i][:], func=RELU)
+            for i, g in enumerate(groups):
+                nc.gpsimd.tensor_tensor(out=zp[t // 2][i][:, t % 2, :], in0=diff[i][:], in1=wins[1][t % 2][:, g], op=ADD)
 
         def weave(u, c, copy):
-            copy(out=zin[c][:, :, 2 * u : 2 * u + 2], in_=zp[u][:, :, chunks[c]].rearrange("p t c -> p c t"))
+            g, c0, c1 = chunks[c]
+            copy(out=zin[c][:, :, 2 * u : 2 * u + 2], in_=zp[u][g][:, :, c0:c1].rearrange("p t c -> p c t"))
 
         scatter(0, 1, relu_out(acc1[:, 128:384], 128, 384, "w2_raw"), 128, 384)
         for s, t in ((1, 0), (1, 1), (0, 2), (1, 2), (0, 3), (1, 3)):
@@ -147,20 +145,22 @@ def tile_picked_bev_max_p_kernel(
                     for c in range(nch):
                         weave(0, c, nc.scalar.copy)
 
-        for h in range(4):
-            join(3, slice(h * 256, (h + 1) * 256))
+        for i, c0, c1 in ((0, 0, 256), (1, 0, 512), (0, 256, 512)):
+            g = slice(groups[i].start + c0, groups[i].start + c1)
+            nc.vector.tensor_tensor(out=zp[1][i][:, 1, c0:c1], in0=wins[0][1][:, g], in1=wins[1][1][:, g], op=MAX)
         for c in range(nch):
-            weave(1, c, nc.scalar.copy if c < 2 else nc.vector.tensor_copy)
-        for c in range(nch):
-            cols = chunks[c]
-            n = cols.stop - cols.start
+            weave(1, c, nc.scalar.copy if c < 3 else nc.vector.tensor_copy)
+        for c in (0, 3, 1, 4, 2):
+            g, c0, c1 = chunks[c]
+            cols = slice(groups[g].start + c0, groups[g].start + c1)
+            n = c1 - c0
             zc = keep.tile([P, n], U32, name=f"zc{c}", align_bytes=64)
             zs = keep.tile([P, n], U8, name=f"zs{c}", align_bytes=64)
             nc.vector.quantize_mx(out=zc[:].bitcast(FP8X4), scales=zs[:], in_=zin[c][:].rearrange("p c t -> p (c t)"))
             acc = psum.tile([P, V], F32, name="acc")
             nc.tensor.matmul_mx(out=acc[:, :n], lhsT=w3w[:].bitcast(FP4X4), lhsT_scale=w3s[:], rhs=zc[:].bitcast(FP8X4), rhs_scale=zs[:], start=True, stop=True)
             res = keep.tile([P, n], F32, name=f"res{c}")
-            if c == nch - 1:
+            if n == 128:
                 nc.vector.tensor_copy(out=res[:], in_=acc[:, :n])
             else:
                 nc.scalar.copy(out=res[:], in_=acc[:, :n])

@@ -38,35 +38,44 @@ def tile_picked_bev_max_p_kernel(
         w3w = keep.tile([P, 2 * N], U8, name="w3w", align_bytes=64)
         w3s = keep.tile([P, N], U8, name="w3s", align_bytes=64)
 
-        nc.gpsimd.memset(xs[:].bitcast(I32), 0)
+        HALF = H // 2
+
+        def load_half(w, h, name, rows):
+            raw = keep.tile([P, PACK, HALF], F32, name=name, tag=name)
+            view = w.rearrange("(p j) c -> p j c", j=PACK)
+            for j0, j1 in rows:
+                nc.sync.dma_start(out=raw[:, j0:j1, :], in_=view[:, j0:j1, h * HALF : (h + 1) * HALF])
+            return raw
+
+        nc.vector.memset(xs[:].bitcast(I32), 0)
         nc.sync.dma_start(offs_t[:], offs)
-        nc.sync.dma_start(near_t[:], near)
-        nc.sync.dma_start(far_t[:], far)
+        w1a = load_half(w1, 0, "w1a", ((0, 2), (2, 4)))
         for q in range(4):
             nc.sync.dma_start(out=xs[32 * q : 32 * q + 4, :].bitcast(I32), in_=x_scales[0, 4 * q : 4 * q + 4, :].bitcast(I32))
-        w1_raw = keep.tile([P, PACK, H], F32, name="w1_raw")
-        nc.sync.dma_start(out=w1_raw[:], in_=w1.rearrange("(p j) c -> p j c", j=PACK))
+        w1b = load_half(w1, 1, "w1b", ((0, 4),))
         nc.sync.dma_start(out=xw[:], in_=x_words[0].rearrange("p n t -> p (n t)").bitcast(I32))
-        w2_raw = keep.tile([P, PACK, H], F32, name="w2_raw", tag="w2_raw")
-        nc.sync.dma_start(out=w2_raw[:], in_=w2.rearrange("(p j) c -> p j c", j=PACK))
-        nc.gpsimd.memset(w3s[:].bitcast(I32), 0)
+        nc.sync.dma_start(near_t[:], near)
+        w2a = load_half(w2, 0, "w2a", ((0, 4),))
+        w2b = load_half(w2, 1, "w2b", ((0, 4),))
+        nc.sync.dma_start(far_t[:], far)
+        nc.vector.memset(w3s[:].bitcast(I32), 0)
         nc.sync.dma_start(out=w3w[:].bitcast(I32), in_=w3_words[0].bitcast(I32))
         for q in range(4):
             nc.sync.dma_start(out=w3s[32 * q : 32 * q + 4, :].bitcast(I32), in_=w3_scales[0, 4 * q : 4 * q + 4, :].bitcast(I32))
 
-        wins = [[keep.tile([P, S], F32, name=f"win{s}_{b}") for b in range(2)] for s in range(2)]
-        for b in range(2):
-            nc.vector.memset(wins[0][b][:], 0.0)
-            nc.scalar.copy(out=wins[1][b][:], in_=wins[0][b][:])
+        win_a = [keep.tile([P, S], F32, name=f"win_a{b}") for b in range(2)]
+        win_e0 = keep.tile([P, S], F32, name="win_e0")
+        nc.vector.memset(win_a[0][:], 0.0)
+        nc.scalar.activation(out=win_a[1][:], in_=win_a[0][:], func=RELU)
+        nc.vector.memset(win_e0[:], 0.0)
 
-        gs = [keep.tile([P, V], U8, name=f"gs{s}", align_bytes=64) for s in range(2)]
-        for s in range(2):
-            nc.vector.tensor_copy(out=gs[s][:], in_=xs[:].indirect(offs_t[:, s * (V // 16) : (s + 1) * (V // 16)]))
+        gs = keep.tile([P, S], U8, name="gs", align_bytes=64)
+        nc.vector.tensor_copy(out=gs[:], in_=xs[:].indirect(offs_t[:]))
 
-        def cast(copy, grouped, raw, m0, m1):
-            copy(
-                out=grouped[:].rearrange("p (t m j) -> p m t j", t=PACK, j=PACK)[:, m0:m1],
-                in_=raw[:].rearrange("p j (m t) -> p m t j", t=PACK)[:, m0:m1],
+        def cast(grouped, raw, h):
+            nc.scalar.copy(
+                out=grouped[:].rearrange("p (t m j) -> p m t j", t=PACK, j=PACK)[:, 64 * h : 64 * (h + 1)],
+                in_=raw[:].rearrange("p j (m t) -> p m t j", t=PACK),
             )
 
         def quant(grouped, t0, t1, name):
@@ -76,43 +85,43 @@ def tile_picked_bev_max_p_kernel(
             nc.vector.quantize_mx(out=codes[:].bitcast(FP8X4), scales=scales[:], in_=grouped[:, t0 * PACK * P : t1 * PACK * P])
             return [(codes[:, (t - t0) * P : (t - t0 + 1) * P], scales[:, (t - t0) * P : (t - t0 + 1) * P]) for t in range(t0, t1)]
 
-        def product(s, wq, v0, v1, tag="acc"):
-            acc = psum.tile([P, V], F32, name=tag, tag=tag)
-            nc.tensor.matmul_mx(out=acc[:, : v1 - v0], lhsT=wq[0].bitcast(FP8X4), lhsT_scale=wq[1], rhs=gw[:, s * V + v0 : s * V + v1].bitcast(FP8X4), rhs_scale=gs[s][:, v0:v1], start=True, stop=True)
-            return acc
+        def product(s, wq, v0, v1):
+            acc = psum.tile([P, V], F32, name="acc", tag="acc")
+            cols = slice(s * V + v0, s * V + v1)
+            nc.tensor.matmul_mx(out=acc[:, : v1 - v0], lhsT=wq[0].bitcast(FP8X4), lhsT_scale=wq[1], rhs=gw[:, cols].bitcast(FP8X4), rhs_scale=gs[:, cols], start=True, stop=True)
+            return acc[:, : v1 - v0]
 
         lists = [near_t, far_t]
 
-        def scatter(s, t, src, v0=0, v1=V):
-            nc.vector.tensor_copy(out=wins[s][t % 2][:].indirect(lists[s][:, v0 // 16 : v1 // 16]), in_=src)
+        def scatter(s, t, src):
+            nc.vector.tensor_copy(out=wins[s][t % 2][:].indirect(lists[s][:]), in_=src[:])
 
-        g1 = keep.tile([P, PACK * H], BF16, name="g1", tag="grouped", align_bytes=64)
-        cast(nc.scalar.copy, g1, w1_raw, 0, 56)
-        cast(nc.vector.tensor_copy, g1, w1_raw, 56, 128)
+        g1 = keep.tile([P, PACK * H], BF16, name="g1", align_bytes=64)
+        cast(g1, w1a, 0)
+        cast(g1, w1b, 1)
         wq1 = quant(g1, 0, 1, "qa0") + quant(g1, 1, 2, "qa1") + quant(g1, 2, 4, "qa2")
 
-        gw = keep.tile([P, S], U32, name="gw", tag="grouped", align_bytes=64)
+        win_e1 = keep.tile([P, S], F32, name="win_e1", tag="w1b")
+        nc.scalar.copy(out=win_e1[:], in_=win_e0[:])
+        wins = [win_a, [win_e0, win_e1]]
+
+        gw = keep.tile([P, S], U32, name="gw", align_bytes=64)
         for v0, v1 in ((0, 256), (256, 512), (512, 1024)):
             nc.vector.tensor_copy(out=gw[:, v0:v1], in_=xw[:].bitcast(U32).indirect(offs_t[:, v0 // 16 : v1 // 16]))
 
-        def relu_out(acc, v0, v1, tag):
-            src = keep.tile([P, v1 - v0], F32, name="src_" + tag, tag=tag)
-            nc.scalar.activation(out=src[:], in_=acc, func=RELU)
-            return src[:]
+        def layer(s, t, wq, tag, pieces=((0, V),)):
+            src = keep.tile([P, V], F32, name="src_" + tag, tag=tag)
+            for v0, v1 in pieces:
+                nc.scalar.activation(out=src[:, v0:v1], in_=product(s, wq, v0, v1), func=RELU)
+            scatter(s, t, src)
 
-        acc = product(0, wq1[0], 0, 256)
-        scatter(0, 0, relu_out(acc[:, :256], 0, 256, "a0a"), 0, 256)
-        acc1 = product(0, wq1[1], 0, V, "held")
-        acc = product(0, wq1[0], 256, V)
-        late = relu_out(acc[:, :256], 256, V, "a0b")
-        scatter(0, 1, relu_out(acc1[:, :128], 0, 128, "a1a"), 0, 128)
-        scatter(0, 0, late, 256, V)
+        layer(0, 0, wq1[0], "s00", ((0, 256), (256, V)))
 
         g2 = keep.tile([P, PACK * H], BF16, name="g2", tag="qa0", align_bytes=64)
-        for h in range(4):
-            cast(nc.scalar.copy, g2, w2_raw, 32 * h, 32 * (h + 1))
-        wq2 = quant(g2, 0, 4, "qe")
-        wq = [wq1, wq2]
+        cast(g2, w2a, 0)
+        cast(g2, w2b, 1)
+        wq = [wq1, quant(g2, 0, 4, "qe")]
+        layer(0, 1, wq1[1], "w2b")
 
         groups = [slice(0, 512), slice(512, 1024)]
         chunks = [(0, 0, 256), (0, 256, 512), (1, 0, 128), (1, 128, 384), (1, 384, 512)]
@@ -132,12 +141,8 @@ def tile_picked_bev_max_p_kernel(
             g, c0, c1 = chunks[c]
             copy(out=zin[c][:, :, 2 * u : 2 * u + 2], in_=zp[u][g][:, :, c0:c1].rearrange("p t c -> p c t"))
 
-        scatter(0, 1, relu_out(acc1[:, 128:384], 128, 384, "w2_raw"), 128, 384)
         for s, t in ((1, 0), (1, 1), (0, 2), (1, 2), (0, 3), (1, 3)):
-            acc = product(s, wq[s][t], 0, V)
-            scatter(s, t, relu_out(acc[:], 0, V, f"s{s}{t}"), 0, V)
-            if (s, t) == (1, 1):
-                scatter(0, 1, relu_out(acc1[:, 384:], 384, V, "s10"), 384, V)
+            layer(s, t, wq[s][t], f"s{s}{t}")
             if s == 1:
                 if t < 3:
                     join_aside(t)

@@ -20,6 +20,18 @@ ADD = mybir.AluOpType.add
 
 P = 128
 PACK = 4
+STRIPE = 16
+HALF = H // 2
+NEAR, FAR = 0, 1
+BANKS = 4
+
+NEAR1_FIRST = 384
+
+GROUPS = (slice(0, 512), slice(512, 1024))
+CHUNKS = ((0, 0, 256), (0, 256, 512), (1, 0, 128), (1, 128, 384), (1, 384, 512))
+SCALAR_CHUNKS = 3
+MAX_PIECES = ((0, 0, 256), (1, 0, 512), (0, 256, 512))
+CHUNK_ORDER = (0, 3, 1, 4, 2)
 
 
 def tile_picked_bev_max_p_kernel(
@@ -28,145 +40,156 @@ def tile_picked_bev_max_p_kernel(
     nc = tc.nc
     with ExitStack() as ctx:
         keep = ctx.enter_context(tc.tile_pool(name="keep", bufs=1))
-        psum = ctx.enter_context(tc.psum_pool(name="psum", bufs=4))
+        psum = ctx.enter_context(tc.psum_pool(name="psum", bufs=BANKS))
 
-        offs_t = keep.tile([P, S // 16], U16, name="offs_t")
-        near_t = keep.tile([P, V // 16], U16, name="near_t")
-        far_t = keep.tile([P, V // 16], U16, name="far_t")
+        offs_t = keep.tile([P, S // STRIPE], U16, name="offs_t")
+        near_t = keep.tile([P, V // STRIPE], U16, name="near_t")
+        far_t = keep.tile([P, V // STRIPE], U16, name="far_t")
         xw = keep.tile([P, T], I32, name="xw", align_bytes=64)
         xs = keep.tile([P, T], U8, name="xs", align_bytes=64)
         w3w = keep.tile([P, 2 * N], U8, name="w3w", align_bytes=64)
         w3s = keep.tile([P, N], U8, name="w3s", align_bytes=64)
 
-        HALF = H // 2
-
-        def load_half(w, h, name, rows):
+        def load_half(w, h, name, row_runs):
             raw = keep.tile([P, PACK, HALF], F32, name=name, tag=name)
             view = w.rearrange("(p j) c -> p j c", j=PACK)
-            for j0, j1 in rows:
+            for j0, j1 in row_runs:
                 nc.sync.dma_start(out=raw[:, j0:j1, :], in_=view[:, j0:j1, h * HALF : (h + 1) * HALF])
             return raw
 
+        def load_scales(tile, scales):
+            for r in range(4):
+                nc.sync.dma_start(out=tile[r:P:32, :].bitcast(I32), in_=scales[0, r:16:4, :].bitcast(I32))
+
         nc.vector.memset(xs[:].bitcast(I32), 0)
-        nc.sync.dma_start(offs_t[:], offs)
         w1a = load_half(w1, 0, "w1a", ((0, 2), (2, 4)))
-        for q in range(4):
-            nc.sync.dma_start(out=xs[32 * q : 32 * q + 4, :].bitcast(I32), in_=x_scales[0, 4 * q : 4 * q + 4, :].bitcast(I32))
-        w1b = load_half(w1, 1, "w1b", ((0, 4),))
+        nc.sync.dma_start(offs_t[:], offs)
+        load_scales(xs, x_scales)
+        w1b = load_half(w1, 1, "w1b", ((0, PACK),))
         nc.sync.dma_start(out=xw[:], in_=x_words[0].rearrange("p n t -> p (n t)").bitcast(I32))
         nc.sync.dma_start(near_t[:], near)
-        w2a = load_half(w2, 0, "w2a", ((0, 4),))
-        w2b = load_half(w2, 1, "w2b", ((0, 4),))
+        w2a = load_half(w2, 0, "w2a", ((0, PACK),))
+        w2b = load_half(w2, 1, "w2b", ((0, PACK),))
         nc.sync.dma_start(far_t[:], far)
         nc.vector.memset(w3s[:].bitcast(I32), 0)
         nc.sync.dma_start(out=w3w[:].bitcast(I32), in_=w3_words[0].bitcast(I32))
-        for q in range(4):
-            nc.sync.dma_start(out=w3s[32 * q : 32 * q + 4, :].bitcast(I32), in_=w3_scales[0, 4 * q : 4 * q + 4, :].bitcast(I32))
+        load_scales(w3s, w3_scales)
 
-        win_a = [keep.tile([P, S], F32, name=f"win_a{b}") for b in range(2)]
-        win_e0 = keep.tile([P, S], F32, name="win_e0")
-        nc.vector.memset(win_a[0][:], 0.0)
-        nc.scalar.activation(out=win_a[1][:], in_=win_a[0][:], func=RELU)
-        nc.vector.memset(win_e0[:], 0.0)
+        win_near = [keep.tile([P, S], F32, name=f"win_a{b}") for b in range(2)]
+        win_far0 = keep.tile([P, S], F32, name="win_e0")
+        nc.vector.memset(win_near[0][:], 0.0)
+        nc.scalar.activation(out=win_near[1][:], in_=win_near[0][:], func=RELU)
+        nc.vector.memset(win_far0[:], 0.0)
 
         gs = keep.tile([P, S], U8, name="gs", align_bytes=64)
         nc.vector.tensor_copy(out=gs[:], in_=xs[:].indirect(offs_t[:]))
 
-        def cast(grouped, raw, h):
+        def round_half(grouped, raw, h):
+            columns = HALF // PACK
             nc.scalar.copy(
-                out=grouped[:].rearrange("p (t m j) -> p m t j", t=PACK, j=PACK)[:, 64 * h : 64 * (h + 1)],
+                out=grouped[:].rearrange("p (t m j) -> p m t j", t=PACK, j=PACK)[:, columns * h : columns * (h + 1)],
                 in_=raw[:].rearrange("p j (m t) -> p m t j", t=PACK),
             )
 
-        def quant(grouped, t0, t1, name):
+        def quantise_tiles(grouped, t0, t1, name):
             n = (t1 - t0) * P
             codes = keep.tile([P, n], U32, name=name + "c", tag=name, align_bytes=64)
             scales = keep.tile([P, n], U8, name=name + "s", align_bytes=64)
             nc.vector.quantize_mx(out=codes[:].bitcast(FP8X4), scales=scales[:], in_=grouped[:, t0 * PACK * P : t1 * PACK * P])
-            return [(codes[:, (t - t0) * P : (t - t0 + 1) * P], scales[:, (t - t0) * P : (t - t0 + 1) * P]) for t in range(t0, t1)]
-
-        def product(s, wq, v0, v1):
-            acc = psum.tile([P, V], F32, name="acc", tag="acc")
-            cols = slice(s * V + v0, s * V + v1)
-            nc.tensor.matmul_mx(out=acc[:, : v1 - v0], lhsT=wq[0].bitcast(FP8X4), lhsT_scale=wq[1], rhs=gw[:, cols].bitcast(FP8X4), rhs_scale=gs[:, cols], start=True, stop=True)
-            return acc[:, : v1 - v0]
-
-        lists = [near_t, far_t]
-
-        def scatter(s, t, src):
-            nc.vector.tensor_copy(out=wins[s][t % 2][:].indirect(lists[s][:]), in_=src[:])
+            return [(codes[:, u * P : (u + 1) * P], scales[:, u * P : (u + 1) * P]) for u in range(t1 - t0)]
 
         g1 = keep.tile([P, PACK * H], BF16, name="g1", align_bytes=64)
-        cast(g1, w1a, 0)
-        cast(g1, w1b, 1)
-        wq1 = quant(g1, 0, 1, "qa0") + quant(g1, 1, 2, "qa1") + quant(g1, 2, 4, "qa2")
+        round_half(g1, w1a, 0)
+        round_half(g1, w1b, 1)
+        wq_near = quantise_tiles(g1, 0, 1, "qa0") + quantise_tiles(g1, 1, 2, "qa1") + quantise_tiles(g1, 2, 4, "qa2")
 
-        win_e1 = keep.tile([P, S], F32, name="win_e1", tag="w1b")
-        nc.scalar.copy(out=win_e1[:], in_=win_e0[:])
-        wins = [win_a, [win_e0, win_e1]]
+        win_far1 = keep.tile([P, S], F32, name="win_e1", tag="w1b")
+        nc.scalar.copy(out=win_far1[:], in_=win_far0[:])
+        wins = [win_near, [win_far0, win_far1]]
+        lists = [near_t, far_t]
 
         gw = keep.tile([P, S], U32, name="gw", align_bytes=64)
-        for v0, v1 in ((0, 256), (256, 512), (512, 1024)):
-            nc.vector.tensor_copy(out=gw[:, v0:v1], in_=xw[:].bitcast(U32).indirect(offs_t[:, v0 // 16 : v1 // 16]))
+        for v0, v1 in ((0, V // 2), (V // 2, V), (V, S)):
+            nc.vector.tensor_copy(out=gw[:, v0:v1], in_=xw[:].bitcast(U32).indirect(offs_t[:, v0 // STRIPE : v1 // STRIPE]))
 
-        def layer(s, t, wq, tag, pieces=((0, V),)):
-            src = keep.tile([P, V], F32, name="src_" + tag, tag=tag)
+        def layer(sensor, t, weights, tag, pieces=((0, V),)):
+            first, last = pieces[0][0], pieces[-1][1]
+            src = keep.tile([P, last - first], F32, name="src_" + tag, tag=tag)
             for v0, v1 in pieces:
-                nc.scalar.activation(out=src[:, v0:v1], in_=product(s, wq, v0, v1), func=RELU)
-            scatter(s, t, src)
+                acc = psum.tile([P, V], F32, name="acc", tag="acc")
+                cols = slice(sensor * V + v0, sensor * V + v1)
+                nc.tensor.matmul_mx(
+                    out=acc[:, : v1 - v0],
+                    lhsT=weights[t][0].bitcast(FP8X4),
+                    lhsT_scale=weights[t][1],
+                    rhs=gw[:, cols].bitcast(FP8X4),
+                    rhs_scale=gs[:, cols],
+                    start=True,
+                    stop=True,
+                )
+                nc.scalar.activation(out=src[:, v0 - first : v1 - first], in_=acc[:, : v1 - v0], func=RELU)
+            nc.vector.tensor_copy(out=wins[sensor][t % 2][:].indirect(lists[sensor][:, first // STRIPE : last // STRIPE]), in_=src[:])
 
-        layer(0, 0, wq1[0], "s00", ((0, 256), (256, V)))
+        layer(NEAR, 0, wq_near, "s00", ((0, V // 2), (V // 2, V)))
 
         g2 = keep.tile([P, PACK * H], BF16, name="g2", tag="qa0", align_bytes=64)
-        cast(g2, w2a, 0)
-        cast(g2, w2b, 1)
-        wq = [wq1, quant(g2, 0, 4, "qe")]
-        layer(0, 1, wq1[1], "w2b")
+        round_half(g2, w2a, 0)
+        round_half(g2, w2b, 1)
+        wq_far = quantise_tiles(g2, 0, PACK, "qe")
+        layer(NEAR, 1, wq_near, "w2b", ((0, V // 2), (V // 2, NEAR1_FIRST)))
 
-        groups = [slice(0, 512), slice(512, 1024)]
-        chunks = [(0, 0, 256), (0, 256, 512), (1, 0, 128), (1, 128, 384), (1, 384, 512)]
-        nch = len(chunks)
-        zp = [[keep.tile([P, 2, g.stop - g.start], BF16, name=f"zp{u}_{g.start}") for g in groups] for u in range(2)]
-        zin = [keep.tile([P, c1 - c0, PACK], BF16, name=f"zin{c}", align_bytes=64) for c, (g, c0, c1) in enumerate(chunks)]
+        zp = [[keep.tile([P, 2, g.stop - g.start], BF16, name=f"zp{u}_{g.start}") for g in GROUPS] for u in range(2)]
+        zin = [keep.tile([P, c1 - c0, PACK], BF16, name=f"zin{c}", align_bytes=64) for c, (group, c0, c1) in enumerate(CHUNKS)]
 
         def join_aside(t):
-            diff = [keep.tile([P, g.stop - g.start], F32, name=f"diff{g.start}") for g in groups]
-            for i, g in enumerate(groups):
-                nc.gpsimd.tensor_tensor(out=diff[i][:], in0=wins[0][t % 2][:, g], in1=wins[1][t % 2][:, g], op=SUB)
+            diff = [keep.tile([P, g.stop - g.start], F32, name=f"diff{g.start}") for g in GROUPS]
+            for i, g in enumerate(GROUPS):
+                nc.gpsimd.tensor_tensor(out=diff[i][:], in0=wins[NEAR][t % 2][:, g], in1=wins[FAR][t % 2][:, g], op=SUB)
                 nc.scalar.activation(out=diff[i][:], in_=diff[i][:], func=RELU)
-            for i, g in enumerate(groups):
-                nc.gpsimd.tensor_tensor(out=zp[t // 2][i][:, t % 2, :], in0=diff[i][:], in1=wins[1][t % 2][:, g], op=ADD)
+            for i, g in enumerate(GROUPS):
+                nc.gpsimd.tensor_tensor(out=zp[t // 2][i][:, t % 2, :], in0=diff[i][:], in1=wins[FAR][t % 2][:, g], op=ADD)
 
-        def weave(u, c, copy):
-            g, c0, c1 = chunks[c]
-            copy(out=zin[c][:, :, 2 * u : 2 * u + 2], in_=zp[u][g][:, :, c0:c1].rearrange("p t c -> p c t"))
+        def interleave(u, c, copy):
+            group, c0, c1 = CHUNKS[c]
+            copy(out=zin[c][:, :, 2 * u : 2 * u + 2], in_=zp[u][group][:, :, c0:c1].rearrange("p t c -> p c t"))
 
-        for s, t in ((1, 0), (1, 1), (0, 2), (1, 2), (0, 3), (1, 3)):
-            layer(s, t, wq[s][t], f"s{s}{t}")
-            if s == 1:
-                if t < 3:
-                    join_aside(t)
-                if t == 1:
-                    for c in range(nch):
-                        weave(0, c, nc.scalar.copy)
+        layer(FAR, 0, wq_far, "s10")
+        layer(NEAR, 1, wq_near, "w2b", ((NEAR1_FIRST, V),))
+        join_aside(0)
+        layer(FAR, 1, wq_far, "s11")
+        join_aside(1)
+        for c in range(len(CHUNKS)):
+            interleave(0, c, nc.scalar.copy)
+        layer(NEAR, 2, wq_near, "s02")
+        layer(FAR, 2, wq_far, "s12")
+        join_aside(2)
+        layer(NEAR, 3, wq_near, "s03")
+        layer(FAR, 3, wq_far, "s13")
 
-        for i, c0, c1 in ((0, 0, 256), (1, 0, 512), (0, 256, 512)):
-            g = slice(groups[i].start + c0, groups[i].start + c1)
-            nc.vector.tensor_tensor(out=zp[1][i][:, 1, c0:c1], in0=wins[0][1][:, g], in1=wins[1][1][:, g], op=MAX)
-        for c in range(nch):
-            weave(1, c, nc.scalar.copy if c < 3 else nc.vector.tensor_copy)
-        for c in (0, 3, 1, 4, 2):
-            g, c0, c1 = chunks[c]
-            cols = slice(groups[g].start + c0, groups[g].start + c1)
+        for group, c0, c1 in MAX_PIECES:
+            cells = slice(GROUPS[group].start + c0, GROUPS[group].start + c1)
+            nc.vector.tensor_tensor(out=zp[1][group][:, 1, c0:c1], in0=wins[NEAR][1][:, cells], in1=wins[FAR][1][:, cells], op=MAX)
+        for c in range(len(CHUNKS)):
+            interleave(1, c, nc.scalar.copy if c < SCALAR_CHUNKS else nc.vector.tensor_copy)
+
+        for c in CHUNK_ORDER:
+            group, c0, c1 = CHUNKS[c]
+            cells = slice(GROUPS[group].start + c0, GROUPS[group].start + c1)
             n = c1 - c0
             zc = keep.tile([P, n], U32, name=f"zc{c}", align_bytes=64)
             zs = keep.tile([P, n], U8, name=f"zs{c}", align_bytes=64)
             nc.vector.quantize_mx(out=zc[:].bitcast(FP8X4), scales=zs[:], in_=zin[c][:].rearrange("p c t -> p (c t)"))
-            acc = psum.tile([P, V], F32, name="acc")
-            nc.tensor.matmul_mx(out=acc[:, :n], lhsT=w3w[:].bitcast(FP4X4), lhsT_scale=w3s[:], rhs=zc[:].bitcast(FP8X4), rhs_scale=zs[:], start=True, stop=True)
+            acc = psum.tile([P, V], F32, name="acc", tag="acc")
+            nc.tensor.matmul_mx(
+                out=acc[:, :n],
+                lhsT=w3w[:].bitcast(FP4X4),
+                lhsT_scale=w3s[:],
+                rhs=zc[:].bitcast(FP8X4),
+                rhs_scale=zs[:],
+                start=True,
+                stop=True,
+            )
             res = keep.tile([P, n], F32, name=f"res{c}")
-            if n == 128:
-                nc.vector.tensor_copy(out=res[:], in_=acc[:, :n])
-            else:
-                nc.scalar.copy(out=res[:], in_=acc[:, :n])
-            nc.sync.dma_start(out=out[:, cols], in_=res[:])
+            empty_bank = nc.vector.tensor_copy if c == CHUNK_ORDER[-1] else nc.scalar.copy
+            empty_bank(out=res[:], in_=acc[:, :n])
+            nc.sync.dma_start(out=out[:, cells], in_=res[:])

@@ -17,11 +17,13 @@ RELU = mybir.ActivationFunctionType.Relu
 MAX = mybir.AluOpType.max
 SUB = mybir.AluOpType.subtract
 ADD = mybir.AluOpType.add
+MULT = mybir.AluOpType.mult
 
 P = 128
 PACK = 4
 STRIPE = 16
 HALF = H // 2
+SCALAR_ROUNDS = 80
 NEAR, FAR = 0, 1
 BANKS = 4
 
@@ -61,11 +63,16 @@ def tile_picked_bev_max_p_kernel(
             for r in range(4):
                 nc.sync.dma_start(out=tile[r:P:32, :].bitcast(I32), in_=scales[0, r:16:4, :].bitcast(I32))
 
-        nc.vector.memset(xs[:].bitcast(I32), 0)
-        w1a = load_half(w1, 0, "w1a", ((0, 2), (2, 4)))
+        xs_words = xs[:].bitcast(I32)
+        nc.vector.memset(xs_words[:, : T // 8], 0)
+        nc.gpsimd.memset(xs_words[:, T // 8 :], 0)
+        w1_rows = w1.rearrange("(p j) c -> p j c", j=PACK)
+        w1a = keep.tile([P, 2, H], F32, name="w1a", tag="w1a")
+        w1b = keep.tile([P, 2, H], F32, name="w1b", tag="w1b")
+        nc.sync.dma_start(out=w1a[:], in_=w1_rows[:, :2, :])
         nc.sync.dma_start(offs_t[:], offs)
         load_scales(xs, x_scales)
-        w1b = load_half(w1, 1, "w1b", ((0, PACK),))
+        nc.sync.dma_start(out=w1b[:], in_=w1_rows[:, 2:, :])
         nc.sync.dma_start(out=xw[:], in_=x_words[0].rearrange("p n t -> p (n t)").bitcast(I32))
         nc.sync.dma_start(near_t[:], near)
         w2a = load_half(w2, 0, "w2a", ((0, PACK),))
@@ -99,8 +106,11 @@ def tile_picked_bev_max_p_kernel(
             return [(codes[:, u * P : (u + 1) * P], scales[:, u * P : (u + 1) * P]) for u in range(t1 - t0)]
 
         g1 = keep.tile([P, PACK * H], BF16, name="g1", align_bytes=64)
-        round_half(g1, w1a, 0)
-        round_half(g1, w1b, 1)
+        for u, raw in enumerate((w1a, w1b)):
+            target = g1[:].rearrange("p (t m j) -> p m t j", t=PACK, j=PACK)[:, :, :, 2 * u : 2 * u + 2]
+            source = raw[:].rearrange("p j (m t) -> p m t j", t=PACK)
+            nc.scalar.copy(out=target[:, :SCALAR_ROUNDS], in_=source[:, :SCALAR_ROUNDS])
+            nc.gpsimd.tensor_scalar(target[:, SCALAR_ROUNDS:], source[:, SCALAR_ROUNDS:], 1.0, 0.0, MULT, ADD)
         wq_near = quantise_tiles(g1, 0, 1, "qa0") + quantise_tiles(g1, 1, 2, "qa1") + quantise_tiles(g1, 2, 4, "qa2")
 
         win_far1 = keep.tile([P, S], F32, name="win_e1", tag="w1b")

@@ -14,8 +14,8 @@ U8 = mybir.dt.uint8
 FP8X4 = mybir.dt.float8_e4m3fn_x4
 FP4X4 = mybir.dt.float4_e2m1fn_x4
 RELU = mybir.ActivationFunctionType.Relu
+COPY = mybir.ActivationFunctionType.Copy
 MAX = mybir.AluOpType.max
-SUB = mybir.AluOpType.subtract
 ADD = mybir.AluOpType.add
 MULT = mybir.AluOpType.mult
 
@@ -25,9 +25,9 @@ STRIPE = 16
 HALF = H // 2
 SCALAR_ROUNDS = 80
 NEAR, FAR = 0, 1
-BANKS = 4
+BANKS = 8
 
-NEAR1_FIRST = 384
+A3_FIRST = 256
 
 GROUPS = (slice(0, 512), slice(512, 1024))
 CHUNKS = ((0, 0, 256), (0, 256, 512), (1, 0, 128), (1, 128, 384), (1, 384, 512))
@@ -82,20 +82,27 @@ def tile_picked_bev_max_p_kernel(
         nc.sync.dma_start(out=w3w[:].bitcast(I32), in_=w3_words[0].bitcast(I32))
         load_scales(w3s, w3_scales)
 
-        win_near = [keep.tile([P, S], F32, name=f"win_a{b}") for b in range(2)]
-        win_far0 = keep.tile([P, S], F32, name="win_e0")
-        nc.vector.memset(win_near[0][:], 0.0)
-        nc.scalar.activation(out=win_near[1][:], in_=win_near[0][:], func=RELU)
-        nc.vector.memset(win_far0[:], 0.0)
+        win_a0 = keep.tile([P, S], F32, name="win_a0")
+        win_a1 = keep.tile([P, S], F32, name="win_a1")
+        win_a3 = keep.tile([P, S], F32, name="win_a3")
+        win_e0 = keep.tile([P, S], F32, name="win_e0")
+        nc.vector.memset(win_a0[:], 0.0)
+        nc.scalar.activation(out=win_a1[:], in_=win_a0[:], func=RELU)
+        nc.vector.memset(win_e0[:], 0.0)
+        nc.vector.memset(win_a3[:], 0.0)
 
         gs = keep.tile([P, S], U8, name="gs", align_bytes=64)
         nc.vector.tensor_copy(out=gs[:], in_=xs[:].indirect(offs_t[:]))
 
         def round_half(grouped, raw, h):
             columns = HALF // PACK
-            nc.scalar.copy(
-                out=grouped[:].rearrange("p (t m j) -> p m t j", t=PACK, j=PACK)[:, columns * h : columns * (h + 1)],
-                in_=raw[:].rearrange("p j (m t) -> p m t j", t=PACK),
+            nc.gpsimd.tensor_scalar(
+                grouped[:].rearrange("p (t m j) -> p m t j", t=PACK, j=PACK)[:, columns * h : columns * (h + 1)],
+                raw[:].rearrange("p j (m t) -> p m t j", t=PACK),
+                1.0,
+                0.0,
+                MULT,
+                ADD,
             )
 
         def quantise_tiles(grouped, t0, t1, name):
@@ -113,74 +120,109 @@ def tile_picked_bev_max_p_kernel(
             nc.gpsimd.tensor_scalar(target[:, SCALAR_ROUNDS:], source[:, SCALAR_ROUNDS:], 1.0, 0.0, MULT, ADD)
         wq_near = quantise_tiles(g1, 0, 1, "qa0") + quantise_tiles(g1, 1, 2, "qa1") + quantise_tiles(g1, 2, 4, "qa2")
 
-        win_far1 = keep.tile([P, S], F32, name="win_e1", tag="w1b")
-        nc.scalar.copy(out=win_far1[:], in_=win_far0[:])
-        wins = [win_near, [win_far0, win_far1]]
+        win_e1 = keep.tile([P, S], F32, name="win_e1", tag="w1b")
+        nc.scalar.copy(out=win_e1[:], in_=win_e0[:])
+        wins = [[win_a0, win_a1, win_a0, win_a3], [win_e0, win_e1, win_e1, win_e0]]
         lists = [near_t, far_t]
 
         gw = keep.tile([P, S], U32, name="gw", align_bytes=64)
         for v0, v1 in ((0, V // 2), (V // 2, V), (V, S)):
             nc.vector.tensor_copy(out=gw[:, v0:v1], in_=xw[:].bitcast(U32).indirect(offs_t[:, v0 // STRIPE : v1 // STRIPE]))
 
-        def layer(sensor, t, weights, tag, pieces=((0, V),)):
-            first, last = pieces[0][0], pieces[-1][1]
-            src = keep.tile([P, last - first], F32, name="src_" + tag, tag=tag)
-            for v0, v1 in pieces:
-                acc = psum.tile([P, V], F32, name="acc", tag="acc")
-                cols = slice(sensor * V + v0, sensor * V + v1)
-                nc.tensor.matmul_mx(
-                    out=acc[:, : v1 - v0],
-                    lhsT=weights[t][0].bitcast(FP8X4),
-                    lhsT_scale=weights[t][1],
-                    rhs=gw[:, cols].bitcast(FP8X4),
-                    rhs_scale=gs[:, cols],
-                    start=True,
-                    stop=True,
-                )
-                nc.scalar.activation(out=src[:, v0 - first : v1 - first], in_=acc[:, : v1 - v0], func=RELU)
-            nc.vector.tensor_copy(out=wins[sensor][t % 2][:].indirect(lists[sensor][:, first // STRIPE : last // STRIPE]), in_=src[:])
+        def product(sensor, t, weights, v0, v1):
+            acc = psum.tile([P, V], F32, name="acc", tag="acc")
+            cols = slice(sensor * V + v0, sensor * V + v1)
+            nc.tensor.matmul_mx(
+                out=acc[:, : v1 - v0],
+                lhsT=weights[t][0].bitcast(FP8X4),
+                lhsT_scale=weights[t][1],
+                rhs=gw[:, cols].bitcast(FP8X4),
+                rhs_scale=gs[:, cols],
+                start=True,
+                stop=True,
+            )
+            return acc
 
-        layer(NEAR, 0, wq_near, "s00", ((0, V // 2), (V // 2, V)))
+        def relu_scalar(values, acc):
+            nc.scalar.activation(out=values, in_=acc, func=RELU)
 
-        g2 = keep.tile([P, PACK * H], BF16, name="g2", tag="qa0", align_bytes=64)
+        def relu_vector(values, acc):
+            nc.vector.tensor_scalar_max(values, acc, 0.0)
+
+        def scatter_vector(sensor, t, v0, v1, values):
+            nc.vector.tensor_copy(out=wins[sensor][t][:].indirect(lists[sensor][:, v0 // STRIPE : v1 // STRIPE]), in_=values)
+
+        def scatter_scalar(sensor, t, v0, v1, values):
+            nc.scalar.activation(out=wins[sensor][t][:].indirect(lists[sensor][:, v0 // STRIPE : v1 // STRIPE]), in_=values, func=COPY)
+
+        def join(t, target, cells):
+            nc.vector.tensor_tensor(out=target, in0=wins[NEAR][t][:, cells], in1=wins[FAR][t][:, cells], op=MAX)
+
+        first, second = slice(0, V // 2), slice(V // 2, V)
+        a0 = keep.tile([P, V], F32, name="a0")
+        a1 = keep.tile([P, V], F32, name="a1")
+        for v in (first, second):
+            relu_scalar(a0[:, v], product(NEAR, 0, wq_near, v.start, v.stop)[:, first])
+            relu_scalar(a1[:, v], product(NEAR, 1, wq_near, v.start, v.stop)[:, first])
+        acc_a3 = product(NEAR, 3, wq_near, 0, V)
+        acc_a2 = product(NEAR, 2, wq_near, 0, V)
+        scatter_vector(NEAR, 0, 0, V, a0[:])
+        a3 = keep.tile([P, A3_FIRST], F32, name="a3")
+        scatter_scalar(NEAR, 1, 0, V // 2, a1[:, first])
+        relu_scalar(a3[:], acc_a3[:, :A3_FIRST])
+        scatter_scalar(NEAR, 1, V // 2, V, a1[:, second])
+        scatter_scalar(NEAR, 3, 0, A3_FIRST, a3[:])
+
+        g2 = keep.tile([P, PACK * H], BF16, name="g2", align_bytes=64)
         round_half(g2, w2a, 0)
         round_half(g2, w2b, 1)
         wq_far = quantise_tiles(g2, 0, PACK, "qe")
-        layer(NEAR, 1, wq_near, "w2b", ((0, V // 2), (V // 2, NEAR1_FIRST)))
+        acc_e1 = product(FAR, 1, wq_far, 0, V)
+        acc_e0 = product(FAR, 0, wq_far, 0, V)
+        acc_e2 = product(FAR, 2, wq_far, 0, V)
+        acc_e3 = product(FAR, 3, wq_far, 0, V)
+        a2 = keep.tile([P, V], F32, name="a2", tag="w2b")
+        e0 = keep.tile([P, V], F32, name="e0")
+        e1 = keep.tile([P, V], F32, name="e1")
+        e2 = keep.tile([P, V], F32, name="e2")
+        relu_vector(a2[:], acc_a2[:])
+        relu_vector(e1[:], acc_e1[:])
+        scatter_vector(FAR, 1, 0, V, e1[:])
+        relu_scalar(e0[:], acc_e0[:])
+        relu_scalar(e2[:, first], acc_e2[:, first])
+        scatter_scalar(FAR, 0, 0, V // 2, e0[:, first])
+        relu_scalar(e2[:, second], acc_e2[:, second])
+        scatter_scalar(FAR, 0, V // 2, V, e0[:, second])
 
-        zp = [[keep.tile([P, 2, g.stop - g.start], BF16, name=f"zp{u}_{g.start}") for g in GROUPS] for u in range(2)]
+        z01 = keep.tile([P, 2, S], BF16, name="z01", tag="z01")
         zin = [keep.tile([P, c1 - c0, PACK], BF16, name=f"zin{c}", align_bytes=64) for c, (group, c0, c1) in enumerate(CHUNKS)]
+        join(1, z01[:, 1, :], slice(0, S))
+        join(0, z01[:, 0, :], slice(0, S))
+        for c, (group, c0, c1) in enumerate(CHUNKS):
+            cells = slice(GROUPS[group].start + c0, GROUPS[group].start + c1)
+            nc.gpsimd.tensor_scalar(zin[c][:, :, :2], z01[:, :, cells].rearrange("p t c -> p c t"), 1.0, 0.0, MULT, ADD)
 
-        def join_aside(t):
-            diff = [keep.tile([P, g.stop - g.start], F32, name=f"diff{g.start}") for g in GROUPS]
-            for i, g in enumerate(GROUPS):
-                nc.gpsimd.tensor_tensor(out=diff[i][:], in0=wins[NEAR][t % 2][:, g], in1=wins[FAR][t % 2][:, g], op=SUB)
-                nc.scalar.activation(out=diff[i][:], in_=diff[i][:], func=RELU)
-            for i, g in enumerate(GROUPS):
-                nc.gpsimd.tensor_tensor(out=zp[t // 2][i][:, t % 2, :], in0=diff[i][:], in1=wins[FAR][t % 2][:, g], op=ADD)
+        late = keep.tile([P, 2 * V - A3_FIRST], F32, name="late", tag="win_a1")
+        a3_rest, e3 = late[:, : V - A3_FIRST], late[:, V - A3_FIRST :]
+        relu_scalar(a3_rest, acc_a3[:, A3_FIRST:])
+        scatter_vector(NEAR, 3, A3_FIRST, V, a3_rest)
+        scatter_vector(NEAR, 2, 0, V, a2[:])
+        scatter_scalar(FAR, 2, 0, V // 2, e2[:, first])
+        relu_scalar(e3, acc_e3[:])
+        scatter_scalar(FAR, 2, V // 2, V, e2[:, second])
+        scatter_scalar(FAR, 3, 0, V // 2, e3[:, first])
+        scatter_scalar(FAR, 3, V // 2, V, e3[:, second])
 
-        def interleave(u, c, copy):
-            group, c0, c1 = CHUNKS[c]
-            copy(out=zin[c][:, :, 2 * u : 2 * u + 2], in_=zp[u][group][:, :, c0:c1].rearrange("p t c -> p c t"))
-
-        layer(FAR, 0, wq_far, "s10")
-        layer(NEAR, 1, wq_near, "w2b", ((NEAR1_FIRST, V),))
-        join_aside(0)
-        layer(FAR, 1, wq_far, "s11")
-        join_aside(1)
-        for c in range(len(CHUNKS)):
-            interleave(0, c, nc.scalar.copy)
-        layer(NEAR, 2, wq_near, "s02")
-        layer(FAR, 2, wq_far, "s12")
-        join_aside(2)
-        layer(NEAR, 3, wq_near, "s03")
-        layer(FAR, 3, wq_far, "s13")
+        z23 = [keep.tile([P, 2, S // 2], BF16, name="z23a"), keep.tile([P, 2, S // 2], BF16, name="z23b", tag="z01")]
+        for group, cells in enumerate(GROUPS):
+            join(2, z23[group][:, 0, :], cells)
 
         for group, c0, c1 in MAX_PIECES:
             cells = slice(GROUPS[group].start + c0, GROUPS[group].start + c1)
-            nc.vector.tensor_tensor(out=zp[1][group][:, 1, c0:c1], in0=wins[NEAR][1][:, cells], in1=wins[FAR][1][:, cells], op=MAX)
-        for c in range(len(CHUNKS)):
-            interleave(1, c, nc.scalar.copy if c < SCALAR_CHUNKS else nc.vector.tensor_copy)
+            join(3, z23[group][:, 1, c0:c1], cells)
+        for c, (group, c0, c1) in enumerate(CHUNKS):
+            copy = nc.scalar.copy if c < SCALAR_CHUNKS else nc.vector.tensor_copy
+            copy(out=zin[c][:, :, 2:], in_=z23[group][:, :, c0:c1].rearrange("p t c -> p c t"))
 
         for c in CHUNK_ORDER:
             group, c0, c1 = CHUNKS[c]

@@ -28,6 +28,7 @@ NEAR, FAR = 0, 1
 BANKS = 8
 
 A3_FIRST = 256
+E3_FIRST = 192
 
 GROUPS = (slice(0, 512), slice(512, 1024))
 CHUNKS = ((0, 0, 256), (0, 256, 512), (1, 0, 128), (1, 128, 384), (1, 384, 512))
@@ -86,10 +87,11 @@ def tile_picked_bev_max_p_kernel(
         win_a1 = keep.tile([P, S], F32, name="win_a1")
         win_a3 = keep.tile([P, S], F32, name="win_a3")
         win_e0 = keep.tile([P, S], F32, name="win_e0")
+        win_e2 = keep.tile([P, S], F32, name="win_e2")
         nc.vector.memset(win_a0[:], 0.0)
         nc.scalar.activation(out=win_a1[:], in_=win_a0[:], func=RELU)
-        nc.vector.memset(win_e0[:], 0.0)
-        nc.vector.memset(win_a3[:], 0.0)
+        for win in (win_e0, win_a3, win_e2):
+            nc.vector.tensor_copy(out=win[:], in_=win_a0[:])
 
         gs = keep.tile([P, S], U8, name="gs", align_bytes=64)
         nc.vector.tensor_copy(out=gs[:], in_=xs[:].indirect(offs_t[:]))
@@ -105,9 +107,9 @@ def tile_picked_bev_max_p_kernel(
                 ADD,
             )
 
-        def quantise_tiles(grouped, t0, t1, name):
+        def quantise_tiles(grouped, t0, t1, name, tag):
             n = (t1 - t0) * P
-            codes = keep.tile([P, n], U32, name=name + "c", tag=name, align_bytes=64)
+            codes = keep.tile([P, n], U32, name=name + "c", tag=tag, align_bytes=64)
             scales = keep.tile([P, n], U8, name=name + "s", align_bytes=64)
             nc.vector.quantize_mx(out=codes[:].bitcast(FP8X4), scales=scales[:], in_=grouped[:, t0 * PACK * P : t1 * PACK * P])
             return [(codes[:, u * P : (u + 1) * P], scales[:, u * P : (u + 1) * P]) for u in range(t1 - t0)]
@@ -118,16 +120,18 @@ def tile_picked_bev_max_p_kernel(
             source = raw[:].rearrange("p j (m t) -> p m t j", t=PACK)
             nc.scalar.copy(out=target[:, :SCALAR_ROUNDS], in_=source[:, :SCALAR_ROUNDS])
             nc.gpsimd.tensor_scalar(target[:, SCALAR_ROUNDS:], source[:, SCALAR_ROUNDS:], 1.0, 0.0, MULT, ADD)
-        wq_near = quantise_tiles(g1, 0, 1, "qa0") + quantise_tiles(g1, 1, 2, "qa1") + quantise_tiles(g1, 2, 4, "qa2")
+        wq_near = quantise_tiles(g1, 0, 2, "qa0", "qa0")
 
         win_e1 = keep.tile([P, S], F32, name="win_e1", tag="w1b")
         nc.scalar.copy(out=win_e1[:], in_=win_e0[:])
-        wins = [[win_a0, win_a1, win_a0, win_a3], [win_e0, win_e1, win_e1, win_e0]]
+        wins = [[win_a0, win_a1, win_a1, win_a3], [win_e0, win_e1, win_e2, win_e1]]
         lists = [near_t, far_t]
 
         gw = keep.tile([P, S], U32, name="gw", align_bytes=64)
         for v0, v1 in ((0, V // 2), (V // 2, V), (V, S)):
             nc.vector.tensor_copy(out=gw[:, v0:v1], in_=xw[:].bitcast(U32).indirect(offs_t[:, v0 // STRIPE : v1 // STRIPE]))
+
+        wq_near = wq_near + quantise_tiles(g1, 2, PACK, "qa2", "xw")
 
         def product(sensor, t, weights, v0, v1):
             acc = psum.tile([P, V], F32, name="acc", tag="acc")
@@ -176,53 +180,54 @@ def tile_picked_bev_max_p_kernel(
         g2 = keep.tile([P, PACK * H], BF16, name="g2", align_bytes=64)
         round_half(g2, w2a, 0)
         round_half(g2, w2b, 1)
-        wq_far = quantise_tiles(g2, 0, PACK, "qe")
-        acc_e1 = product(FAR, 1, wq_far, 0, V)
+        wq_far = quantise_tiles(g2, 0, 1, "qe0", "qe0") + quantise_tiles(g2, 1, PACK, "qe1", "qe1")
         acc_e0 = product(FAR, 0, wq_far, 0, V)
+        acc_e1 = product(FAR, 1, wq_far, 0, V)
         acc_e2 = product(FAR, 2, wq_far, 0, V)
         acc_e3 = product(FAR, 3, wq_far, 0, V)
         a2 = keep.tile([P, V], F32, name="a2", tag="w2b")
         e0 = keep.tile([P, V], F32, name="e0")
         e1 = keep.tile([P, V], F32, name="e1")
         e2 = keep.tile([P, V], F32, name="e2")
-        relu_vector(a2[:], acc_a2[:])
-        relu_vector(e1[:], acc_e1[:])
-        scatter_vector(FAR, 1, 0, V, e1[:])
-        relu_scalar(e0[:], acc_e0[:])
+        e3 = keep.tile([P, V], F32, name="e3")
+        relu_vector(a2[:, first], acc_a2[:, first])
+        relu_vector(e0[:], acc_e0[:])
+        relu_vector(a2[:, second], acc_a2[:, second])
+        scatter_vector(FAR, 0, 0, V, e0[:])
+        relu_vector(e3[:], acc_e3[:])
+        relu_scalar(e1[:], acc_e1[:])
         relu_scalar(e2[:, first], acc_e2[:, first])
-        scatter_scalar(FAR, 0, 0, V // 2, e0[:, first])
+        scatter_scalar(FAR, 1, 0, V // 2, e1[:, first])
         relu_scalar(e2[:, second], acc_e2[:, second])
-        scatter_scalar(FAR, 0, V // 2, V, e0[:, second])
+        scatter_scalar(FAR, 1, V // 2, V, e1[:, second])
 
         z01 = keep.tile([P, 2, S], BF16, name="z01", tag="z01")
         zin = [keep.tile([P, c1 - c0, PACK], BF16, name=f"zin{c}", align_bytes=64) for c, (group, c0, c1) in enumerate(CHUNKS)]
-        join(1, z01[:, 1, :], slice(0, S))
         join(0, z01[:, 0, :], slice(0, S))
+        join(1, z01[:, 1, :], slice(0, S))
         for c, (group, c0, c1) in enumerate(CHUNKS):
             cells = slice(GROUPS[group].start + c0, GROUPS[group].start + c1)
             nc.gpsimd.tensor_scalar(zin[c][:, :, :2], z01[:, :, cells].rearrange("p t c -> p c t"), 1.0, 0.0, MULT, ADD)
 
-        late = keep.tile([P, 2 * V - A3_FIRST], F32, name="late", tag="win_a1")
-        a3_rest, e3 = late[:, : V - A3_FIRST], late[:, V - A3_FIRST :]
-        relu_scalar(a3_rest, acc_a3[:, A3_FIRST:])
-        scatter_vector(NEAR, 3, A3_FIRST, V, a3_rest)
+        a3_rest = keep.tile([P, V - A3_FIRST], F32, name="a3_rest", tag="e1")
+        scatter_vector(FAR, 3, 0, E3_FIRST, e3[:, :E3_FIRST])
         scatter_vector(NEAR, 2, 0, V, a2[:])
         scatter_scalar(FAR, 2, 0, V // 2, e2[:, first])
-        relu_scalar(e3, acc_e3[:])
+        relu_scalar(a3_rest[:], acc_a3[:, A3_FIRST:])
         scatter_scalar(FAR, 2, V // 2, V, e2[:, second])
-        scatter_scalar(FAR, 3, 0, V // 2, e3[:, first])
-        scatter_scalar(FAR, 3, V // 2, V, e3[:, second])
+        scatter_scalar(NEAR, 3, A3_FIRST, V, a3_rest[:])
+        scatter_scalar(FAR, 3, E3_FIRST, V, e3[:, E3_FIRST:])
 
-        z23 = [keep.tile([P, 2, S // 2], BF16, name="z23a"), keep.tile([P, 2, S // 2], BF16, name="z23b", tag="z01")]
-        for group, cells in enumerate(GROUPS):
-            join(2, z23[group][:, 0, :], cells)
+        z23 = keep.tile([P, 2, S], BF16, name="z23", tag="z01")
+        join(2, z23[:, 0, :], slice(0, S))
 
         for group, c0, c1 in MAX_PIECES:
             cells = slice(GROUPS[group].start + c0, GROUPS[group].start + c1)
-            join(3, z23[group][:, 1, c0:c1], cells)
+            join(3, z23[:, 1, cells], cells)
         for c, (group, c0, c1) in enumerate(CHUNKS):
             copy = nc.scalar.copy if c < SCALAR_CHUNKS else nc.vector.tensor_copy
-            copy(out=zin[c][:, :, 2:], in_=z23[group][:, :, c0:c1].rearrange("p t c -> p c t"))
+            cells = slice(GROUPS[group].start + c0, GROUPS[group].start + c1)
+            copy(out=zin[c][:, :, 2:], in_=z23[:, :, cells].rearrange("p t c -> p c t"))
 
         for c in CHUNK_ORDER:
             group, c0, c1 = CHUNKS[c]

@@ -120,7 +120,7 @@ def tile_picked_bev_max_p_kernel(
             source = raw[:].rearrange("p j (m t) -> p m t j", t=PACK)
             nc.scalar.copy(out=target[:, :SCALAR_ROUNDS], in_=source[:, :SCALAR_ROUNDS])
             nc.gpsimd.tensor_scalar(target[:, SCALAR_ROUNDS:], source[:, SCALAR_ROUNDS:], 1.0, 0.0, MULT, ADD)
-        wq_near = quantise_tiles(g1, 0, 2, "qa0", "qa0")
+        wq_near = quantise_tiles(g1, 0, PACK, "qa", "qa")
 
         win_e1 = keep.tile([P, S], F32, name="win_e1", tag="w1b")
         nc.scalar.copy(out=win_e1[:], in_=win_e0[:])
@@ -130,8 +130,6 @@ def tile_picked_bev_max_p_kernel(
         gw = keep.tile([P, S], U32, name="gw", align_bytes=64)
         for v0, v1 in ((0, V // 2), (V // 2, V), (V, S)):
             nc.vector.tensor_copy(out=gw[:, v0:v1], in_=xw[:].bitcast(U32).indirect(offs_t[:, v0 // STRIPE : v1 // STRIPE]))
-
-        wq_near = wq_near + quantise_tiles(g1, 2, PACK, "qa2", "xw")
 
         def product(sensor, t, weights, v0, v1):
             acc = psum.tile([P, V], F32, name="acc", tag="acc")

@@ -28,13 +28,12 @@ NEAR, FAR = 0, 1
 BANKS = 8
 
 A3_FIRST = 256
-E3_FIRST = 192
+E3_FIRST = 224
 
-GROUPS = (slice(0, 512), slice(512, 1024))
-CHUNKS = ((0, 0, 256), (0, 256, 512), (1, 0, 128), (1, 128, 384), (1, 384, 512))
-SCALAR_CHUNKS = 3
-MAX_PIECES = ((0, 0, 256), (1, 0, 512), (0, 256, 512))
-CHUNK_ORDER = (0, 3, 1, 4, 2)
+CHUNKS = (slice(0, 256), slice(256, 512), slice(512, 640), slice(640, 768), slice(768, 1024))
+SCALAR_CHUNKS = 4
+MAX_PIECES = ((2, slice(0, 512)), (3, slice(0, 256)), (3, slice(256, 512)), (2, slice(512, 1024)), (3, slice(512, 1024)))
+CHUNK_ORDER = (0, 1, 4, 2, 3)
 
 
 def tile_picked_bev_max_p_kernel(
@@ -120,7 +119,7 @@ def tile_picked_bev_max_p_kernel(
             source = raw[:].rearrange("p j (m t) -> p m t j", t=PACK)
             nc.scalar.copy(out=target[:, :SCALAR_ROUNDS], in_=source[:, :SCALAR_ROUNDS])
             nc.gpsimd.tensor_scalar(target[:, SCALAR_ROUNDS:], source[:, SCALAR_ROUNDS:], 1.0, 0.0, MULT, ADD)
-        wq_near = quantise_tiles(g1, 0, PACK, "qa", "qa")
+        wq_near = quantise_tiles(g1, 0, 2, "qa0", "qa0")
 
         win_e1 = keep.tile([P, S], F32, name="win_e1", tag="w1b")
         nc.scalar.copy(out=win_e1[:], in_=win_e0[:])
@@ -130,6 +129,8 @@ def tile_picked_bev_max_p_kernel(
         gw = keep.tile([P, S], U32, name="gw", align_bytes=64)
         for v0, v1 in ((0, V // 2), (V // 2, V), (V, S)):
             nc.vector.tensor_copy(out=gw[:, v0:v1], in_=xw[:].bitcast(U32).indirect(offs_t[:, v0 // STRIPE : v1 // STRIPE]))
+
+        wq_near = wq_near + quantise_tiles(g1, 2, PACK, "qa2", "xw")
 
         def product(sensor, t, weights, v0, v1):
             acc = psum.tile([P, V], F32, name="acc", tag="acc")
@@ -200,11 +201,10 @@ def tile_picked_bev_max_p_kernel(
         scatter_scalar(FAR, 1, V // 2, V, e1[:, second])
 
         z01 = keep.tile([P, 2, S], BF16, name="z01", tag="z01")
-        zin = [keep.tile([P, c1 - c0, PACK], BF16, name=f"zin{c}", align_bytes=64) for c, (group, c0, c1) in enumerate(CHUNKS)]
+        zin = [keep.tile([P, cells.stop - cells.start, PACK], BF16, name=f"zin{c}", align_bytes=64) for c, cells in enumerate(CHUNKS)]
         join(0, z01[:, 0, :], slice(0, S))
         join(1, z01[:, 1, :], slice(0, S))
-        for c, (group, c0, c1) in enumerate(CHUNKS):
-            cells = slice(GROUPS[group].start + c0, GROUPS[group].start + c1)
+        for c, cells in enumerate(CHUNKS):
             nc.gpsimd.tensor_scalar(zin[c][:, :, :2], z01[:, :, cells].rearrange("p t c -> p c t"), 1.0, 0.0, MULT, ADD)
 
         a3_rest = keep.tile([P, V - A3_FIRST], F32, name="a3_rest", tag="e1")
@@ -217,20 +217,15 @@ def tile_picked_bev_max_p_kernel(
         scatter_scalar(FAR, 3, E3_FIRST, V, e3[:, E3_FIRST:])
 
         z23 = keep.tile([P, 2, S], BF16, name="z23", tag="z01")
-        join(2, z23[:, 0, :], slice(0, S))
-
-        for group, c0, c1 in MAX_PIECES:
-            cells = slice(GROUPS[group].start + c0, GROUPS[group].start + c1)
-            join(3, z23[:, 1, cells], cells)
-        for c, (group, c0, c1) in enumerate(CHUNKS):
+        for t, cells in MAX_PIECES:
+            join(t, z23[:, t - 2, cells], cells)
+        for c, cells in enumerate(CHUNKS):
             copy = nc.scalar.copy if c < SCALAR_CHUNKS else nc.vector.tensor_copy
-            cells = slice(GROUPS[group].start + c0, GROUPS[group].start + c1)
             copy(out=zin[c][:, :, 2:], in_=z23[:, :, cells].rearrange("p t c -> p c t"))
 
         for c in CHUNK_ORDER:
-            group, c0, c1 = CHUNKS[c]
-            cells = slice(GROUPS[group].start + c0, GROUPS[group].start + c1)
-            n = c1 - c0
+            cells = CHUNKS[c]
+            n = cells.stop - cells.start
             zc = keep.tile([P, n], U32, name=f"zc{c}", align_bytes=64)
             zs = keep.tile([P, n], U8, name=f"zs{c}", align_bytes=64)
             nc.vector.quantize_mx(out=zc[:].bitcast(FP8X4), scales=zs[:], in_=zin[c][:].rearrange("p c t -> p (c t)"))

@@ -27,8 +27,9 @@ SCALAR_ROUNDS = 80
 NEAR, FAR = 0, 1
 BANKS = 8
 
-A3_FIRST = 256
-E3_FIRST = 224
+A3_FIRST = 224
+E3_FIRST = 256
+E2_FIRST = 384
 
 CHUNKS = (slice(0, 256), slice(256, 512), slice(512, 640), slice(640, 768), slice(768, 1024))
 SCALAR_CHUNKS = 4
@@ -123,14 +124,12 @@ def tile_picked_bev_max_p_kernel(
 
         win_e1 = keep.tile([P, S], F32, name="win_e1", tag="w1b")
         nc.scalar.copy(out=win_e1[:], in_=win_e0[:])
-        wins = [[win_a0, win_a1, win_a1, win_a3], [win_e0, win_e1, win_e2, win_e1]]
+        wins = [[win_a0, win_a1, win_a0, win_a3], [win_e0, win_e1, win_e2, win_e0]]
         lists = [near_t, far_t]
 
         gw = keep.tile([P, S], U32, name="gw", align_bytes=64)
         for v0, v1 in ((0, V // 2), (V // 2, V), (V, S)):
             nc.vector.tensor_copy(out=gw[:, v0:v1], in_=xw[:].bitcast(U32).indirect(offs_t[:, v0 // STRIPE : v1 // STRIPE]))
-
-        wq_near = wq_near + quantise_tiles(g1, 2, PACK, "qa2", "xw")
 
         def product(sensor, t, weights, v0, v1):
             acc = psum.tile([P, V], F32, name="acc", tag="acc")
@@ -164,14 +163,17 @@ def tile_picked_bev_max_p_kernel(
         first, second = slice(0, V // 2), slice(V // 2, V)
         a0 = keep.tile([P, V], F32, name="a0")
         a1 = keep.tile([P, V], F32, name="a1")
-        for v in (first, second):
-            relu_scalar(a0[:, v], product(NEAR, 0, wq_near, v.start, v.stop)[:, first])
-            relu_scalar(a1[:, v], product(NEAR, 1, wq_near, v.start, v.stop)[:, first])
+        relu_scalar(a0[:, first], product(NEAR, 0, wq_near, 0, V // 2)[:, first])
+        relu_scalar(a1[:, first], product(NEAR, 1, wq_near, 0, V // 2)[:, first])
+        relu_scalar(a0[:, second], product(NEAR, 0, wq_near, V // 2, V)[:, first])
+        acc_a1 = product(NEAR, 1, wq_near, V // 2, V)
+        wq_near = wq_near + quantise_tiles(g1, 2, PACK, "qa2", "qa0")
         acc_a3 = product(NEAR, 3, wq_near, 0, V)
         acc_a2 = product(NEAR, 2, wq_near, 0, V)
         scatter_vector(NEAR, 0, 0, V, a0[:])
         a3 = keep.tile([P, A3_FIRST], F32, name="a3")
         scatter_scalar(NEAR, 1, 0, V // 2, a1[:, first])
+        relu_scalar(a1[:, second], acc_a1[:, first])
         relu_scalar(a3[:], acc_a3[:, :A3_FIRST])
         scatter_scalar(NEAR, 1, V // 2, V, a1[:, second])
         scatter_scalar(NEAR, 3, 0, A3_FIRST, a3[:])
@@ -181,24 +183,24 @@ def tile_picked_bev_max_p_kernel(
         round_half(g2, w2b, 1)
         wq_far = quantise_tiles(g2, 0, 1, "qe0", "qe0") + quantise_tiles(g2, 1, PACK, "qe1", "qe1")
         acc_e0 = product(FAR, 0, wq_far, 0, V)
-        acc_e1 = product(FAR, 1, wq_far, 0, V)
+        acc_e1 = [product(FAR, 1, wq_far, v.start, v.stop) for v in (first, second)]
         acc_e2 = product(FAR, 2, wq_far, 0, V)
         acc_e3 = product(FAR, 3, wq_far, 0, V)
         a2 = keep.tile([P, V], F32, name="a2", tag="w2b")
         e0 = keep.tile([P, V], F32, name="e0")
-        e1 = keep.tile([P, V], F32, name="e1")
-        e2 = keep.tile([P, V], F32, name="e2")
+        e1 = [keep.tile([P, V // 2], F32, name=f"e1{h}", tag=f"e1{h}") for h in range(2)]
+        e2 = keep.tile([P, E2_FIRST], F32, name="e2")
         e3 = keep.tile([P, V], F32, name="e3")
         relu_vector(a2[:, first], acc_a2[:, first])
         relu_vector(e0[:], acc_e0[:])
         relu_vector(a2[:, second], acc_a2[:, second])
         scatter_vector(FAR, 0, 0, V, e0[:])
         relu_vector(e3[:], acc_e3[:])
-        relu_scalar(e1[:], acc_e1[:])
-        relu_scalar(e2[:, first], acc_e2[:, first])
-        scatter_scalar(FAR, 1, 0, V // 2, e1[:, first])
-        relu_scalar(e2[:, second], acc_e2[:, second])
-        scatter_scalar(FAR, 1, V // 2, V, e1[:, second])
+        relu_scalar(e1[0][:], acc_e1[0][:, first])
+        relu_scalar(e1[1][:], acc_e1[1][:, first])
+        scatter_scalar(FAR, 1, 0, V // 2, e1[0][:])
+        relu_scalar(e2[:], acc_e2[:, :E2_FIRST])
+        scatter_scalar(FAR, 1, V // 2, V, e1[1][:])
 
         z01 = keep.tile([P, 2, S], BF16, name="z01", tag="z01")
         zin = [keep.tile([P, cells.stop - cells.start, PACK], BF16, name=f"zin{c}", align_bytes=64) for c, cells in enumerate(CHUNKS)]
@@ -207,25 +209,32 @@ def tile_picked_bev_max_p_kernel(
         for c, cells in enumerate(CHUNKS):
             nc.gpsimd.tensor_scalar(zin[c][:, :, :2], z01[:, :, cells].rearrange("p t c -> p c t"), 1.0, 0.0, MULT, ADD)
 
-        a3_rest = keep.tile([P, V - A3_FIRST], F32, name="a3_rest", tag="e1")
-        scatter_vector(FAR, 3, 0, E3_FIRST, e3[:, :E3_FIRST])
+        late = keep.tile([P, 2 * V - E2_FIRST - A3_FIRST], F32, name="late", tag="win_a1")
+        e2_rest, a3_rest = late[:, : V - E2_FIRST], late[:, V - E2_FIRST :]
+        scatter_scalar(FAR, 2, 0, E2_FIRST, e2[:])
+        scatter_scalar(FAR, 3, 0, E3_FIRST, e3[:, :E3_FIRST])
         scatter_vector(NEAR, 2, 0, V, a2[:])
-        scatter_scalar(FAR, 2, 0, V // 2, e2[:, first])
-        relu_scalar(a3_rest[:], acc_a3[:, A3_FIRST:])
-        scatter_scalar(FAR, 2, V // 2, V, e2[:, second])
-        scatter_scalar(NEAR, 3, A3_FIRST, V, a3_rest[:])
-        scatter_scalar(FAR, 3, E3_FIRST, V, e3[:, E3_FIRST:])
+        scatter_vector(FAR, 3, E3_FIRST, V, e3[:, E3_FIRST:])
+        relu_scalar(e2_rest, acc_e2[:, E2_FIRST:])
+        relu_scalar(a3_rest, acc_a3[:, A3_FIRST:])
+        scatter_scalar(FAR, 2, E2_FIRST, V, e2_rest)
+        scatter_scalar(NEAR, 3, A3_FIRST, V, a3_rest)
 
         z23 = keep.tile([P, 2, S], BF16, name="z23", tag="z01")
         for t, cells in MAX_PIECES:
             join(t, z23[:, t - 2, cells], cells)
-        for c, cells in enumerate(CHUNKS):
-            copy = nc.scalar.copy if c < SCALAR_CHUNKS else nc.vector.tensor_copy
-            copy(out=zin[c][:, :, 2:], in_=z23[:, :, cells].rearrange("p t c -> p c t"))
+
+        def interleave(c, copy):
+            copy(out=zin[c][:, :, 2:], in_=z23[:, :, CHUNKS[c]].rearrange("p t c -> p c t"))
+
+        for c in range(SCALAR_CHUNKS):
+            interleave(c, nc.scalar.copy)
 
         for c in CHUNK_ORDER:
             cells = CHUNKS[c]
             n = cells.stop - cells.start
+            if c == CHUNK_ORDER[1]:
+                interleave(SCALAR_CHUNKS, nc.vector.tensor_copy)
             zc = keep.tile([P, n], U32, name=f"zc{c}", align_bytes=64)
             zs = keep.tile([P, n], U8, name=f"zs{c}", align_bytes=64)
             nc.vector.quantize_mx(out=zc[:].bitcast(FP8X4), scales=zs[:], in_=zin[c][:].rearrange("p c t -> p (c t)"))

@@ -203,11 +203,11 @@ def tile_picked_bev_max_p_kernel(
         scatter_scalar(FAR, 1, V // 2, V, e1[1][:])
 
         z01 = keep.tile([P, 2, S], BF16, name="z01", tag="z01")
-        zin = [keep.tile([P, cells.stop - cells.start, PACK], BF16, name=f"zin{c}", align_bytes=64) for c, cells in enumerate(CHUNKS)]
+        woven = keep.tile([P, S * PACK], BF16, name="woven", align_bytes=64)
+        zin = [woven[:, PACK * cells.start : PACK * cells.stop].rearrange("p (c t) -> p c t", t=PACK) for cells in CHUNKS]
         join(0, z01[:, 0, :], slice(0, S))
         join(1, z01[:, 1, :], slice(0, S))
-        for c, cells in enumerate(CHUNKS):
-            nc.gpsimd.tensor_scalar(zin[c][:, :, :2], z01[:, :, cells].rearrange("p t c -> p c t"), 1.0, 0.0, MULT, ADD)
+        nc.gpsimd.tensor_scalar(woven[:].rearrange("p (c t) -> p c t", t=PACK)[:, :, :2], z01[:].rearrange("p t c -> p c t"), 1.0, 0.0, MULT, ADD)
 
         late = keep.tile([P, 2 * V - E2_FIRST - A3_FIRST], F32, name="late", tag="win_a1")
         e2_rest, a3_rest = late[:, : V - E2_FIRST], late[:, V - E2_FIRST :]
@@ -237,7 +237,7 @@ def tile_picked_bev_max_p_kernel(
                 interleave(SCALAR_CHUNKS, nc.vector.tensor_copy)
             zc = keep.tile([P, n], U32, name=f"zc{c}", align_bytes=64)
             zs = keep.tile([P, n], U8, name=f"zs{c}", align_bytes=64)
-            nc.vector.quantize_mx(out=zc[:].bitcast(FP8X4), scales=zs[:], in_=zin[c][:].rearrange("p c t -> p (c t)"))
+            nc.vector.quantize_mx(out=zc[:].bitcast(FP8X4), scales=zs[:], in_=woven[:, PACK * cells.start : PACK * cells.stop])
             acc = psum.tile([P, V], F32, name="acc", tag="acc")
             nc.tensor.matmul_mx(
                 out=acc[:, :n],

@@ -23,7 +23,7 @@ P = 128
 PACK = 4
 STRIPE = 16
 HALF = H // 2
-SCALAR_ROUNDS = 80
+SCALAR_ROUNDS = 88
 NEAR, FAR = 0, 1
 BANKS = 8
 
@@ -90,8 +90,10 @@ def tile_picked_bev_max_p_kernel(
         win_e2 = keep.tile([P, S], F32, name="win_e2")
         nc.vector.memset(win_a0[:], 0.0)
         nc.scalar.activation(out=win_a1[:], in_=win_a0[:], func=RELU)
-        for win in (win_e0, win_a3, win_e2):
+        for win in (win_e0, win_a3):
             nc.vector.tensor_copy(out=win[:], in_=win_a0[:])
+        nc.gpsimd.tensor_scalar(win_e2[:, :P], win_a0[:, :P], 1.0, 0.0, MULT, ADD)
+        nc.vector.tensor_copy(out=win_e2[:, P:], in_=win_a0[:, P:])
 
         gs = keep.tile([P, S], U8, name="gs", align_bytes=64)
         nc.vector.tensor_copy(out=gs[:], in_=xs[:].indirect(offs_t[:]))

from contextlib import ExitStack

import concourse.mybir as mybir

K, T, S, H, N, V = 512, 2048, 1024, 512, 128, 512
FLOPS = 2 * K * H * V * 2 + 2 * H * N * S

F32 = mybir.dt.float32
BF16 = mybir.dt.bfloat16
I32 = mybir.dt.int32
U32 = mybir.dt.uint32
U16 = mybir.dt.uint16
U8 = mybir.dt.uint8
FP8X4 = mybir.dt.float8_e4m3fn_x4
FP4X4 = mybir.dt.float4_e2m1fn_x4
RELU = mybir.ActivationFunctionType.Relu
COPY = mybir.ActivationFunctionType.Copy
MAX = mybir.AluOpType.max
ADD = mybir.AluOpType.add
MULT = mybir.AluOpType.mult

P = 128
PACK = 4
STRIPE = 16
HALF = H // 2
SCALAR_ROUNDS = 88
NEAR, FAR = 0, 1
BANKS = 8

A3_FIRST = 224
E3_FIRST = 256
E2_FIRST = 384

CHUNKS = (slice(0, 256), slice(256, 512), slice(512, 640), slice(640, 768), slice(768, 1024))
SCALAR_CHUNKS = 4
MAX_PIECES = ((2, slice(0, 512)), (3, slice(0, 256)), (3, slice(256, 512)), (2, slice(512, 1024)), (3, slice(512, 1024)))
CHUNK_ORDER = (0, 1, 4, 2, 3)


def tile_picked_bev_max_p_kernel(
    tc, x_words, x_scales, w1, w2, w3_words, w3_scales, offs, near, far, out
):
    nc = tc.nc
    with ExitStack() as ctx:
        keep = ctx.enter_context(tc.tile_pool(name="keep", bufs=1))
        psum = ctx.enter_context(tc.psum_pool(name="psum", bufs=BANKS))

        offs_t = keep.tile([P, S // STRIPE], U16, name="offs_t")
        near_t = keep.tile([P, V // STRIPE], U16, name="near_t")
        far_t = keep.tile([P, V // STRIPE], U16, name="far_t")
        xw = keep.tile([P, T], I32, name="xw", align_bytes=64)
        xs = keep.tile([P, T], U8, name="xs", align_bytes=64)
        w3w = keep.tile([P, 2 * N], U8, name="w3w", align_bytes=64)
        w3s = keep.tile([P, N], U8, name="w3s", align_bytes=64)

        def load_half(w, h, name, row_runs):
            raw = keep.tile([P, PACK, HALF], F32, name=name, tag=name)
            view = w.rearrange("(p j) c -> p j c", j=PACK)
            for j0, j1 in row_runs:
                nc.sync.dma_start(out=raw[:, j0:j1, :], in_=view[:, j0:j1, h * HALF : (h + 1) * HALF])
            return raw

        def load_scales(tile, scales):
            for r in range(4):
                nc.sync.dma_start(out=tile[r:P:32, :].bitcast(I32), in_=scales[0, r:16:4, :].bitcast(I32))

        xs_words = xs[:].bitcast(I32)
        nc.vector.memset(xs_words[:, : T // 8], 0)
        nc.gpsimd.memset(xs_words[:, T // 8 :], 0)
        w1_rows = w1.rearrange("(p j) c -> p j c", j=PACK)
        w1a = keep.tile([P, 2, H], F32, name="w1a", tag="w1a")
        w1b = keep.tile([P, 2, H], F32, name="w1b", tag="w1b")
        nc.sync.dma_start(out=w1a[:], in_=w1_rows[:, :2, :])
        nc.sync.dma_start(offs_t[:], offs)
        load_scales(xs, x_scales)
        nc.sync.dma_start(out=w1b[:], in_=w1_rows[:, 2:, :])
        nc.sync.dma_start(out=xw[:], in_=x_words[0].rearrange("p n t -> p (n t)").bitcast(I32))
        nc.sync.dma_start(near_t[:], near)
        w2a = load_half(w2, 0, "w2a", ((0, PACK),))
        w2b = load_half(w2, 1, "w2b", ((0, PACK),))
        nc.sync.dma_start(far_t[:], far)
        nc.vector.memset(w3s[:].bitcast(I32), 0)
        nc.sync.dma_start(out=w3w[:].bitcast(I32), in_=w3_words[0].bitcast(I32))
        load_scales(w3s, w3_scales)

        win_a0 = keep.tile([P, S], F32, name="win_a0")
        win_a1 = keep.tile([P, S], F32, name="win_a1")
        win_a3 = keep.tile([P, S], F32, name="win_a3")
        win_e0 = keep.tile([P, S], F32, name="win_e0")
        win_e2 = keep.tile([P, S], F32, name="win_e2")
        nc.vector.memset(win_a0[:], 0.0)
        nc.scalar.activation(out=win_a1[:], in_=win_a0[:], func=RELU)
        for win in (win_e0, win_a3):
            nc.vector.tensor_copy(out=win[:], in_=win_a0[:])
        nc.gpsimd.tensor_scalar(win_e2[:, :P], win_a0[:, :P], 1.0, 0.0, MULT, ADD)
        nc.vector.tensor_copy(out=win_e2[:, P:], in_=win_a0[:, P:])

        gs = keep.tile([P, S], U8, name="gs", align_bytes=64)
        nc.vector.tensor_copy(out=gs[:], in_=xs[:].indirect(offs_t[:]))

        def round_half(grouped, raw, h):
            columns = HALF // PACK
            nc.gpsimd.tensor_scalar(
                grouped[:].rearrange("p (t m j) -> p m t j", t=PACK, j=PACK)[:, columns * h : columns * (h + 1)],
                raw[:].rearrange("p j (m t) -> p m t j", t=PACK),
                1.0,
                0.0,
                MULT,
                ADD,
            )

        def quantise_tiles(grouped, t0, t1, name, tag):
            n = (t1 - t0) * P
            codes = keep.tile([P, n], U32, name=name + "c", tag=tag, align_bytes=64)
            scales = keep.tile([P, n], U8, name=name + "s", align_bytes=64)
            nc.vector.quantize_mx(out=codes[:].bitcast(FP8X4), scales=scales[:], in_=grouped[:, t0 * PACK * P : t1 * PACK * P])
            return [(codes[:, u * P : (u + 1) * P], scales[:, u * P : (u + 1) * P]) for u in range(t1 - t0)]

        g1 = keep.tile([P, PACK * H], BF16, name="g1", align_bytes=64)
        for u, raw in enumerate((w1a, w1b)):
            target = g1[:].rearrange("p (t m j) -> p m t j", t=PACK, j=PACK)[:, :, :, 2 * u : 2 * u + 2]
            source = raw[:].rearrange("p j (m t) -> p m t j", t=PACK)
            nc.scalar.copy(out=target[:, :SCALAR_ROUNDS], in_=source[:, :SCALAR_ROUNDS])
            nc.gpsimd.tensor_scalar(target[:, SCALAR_ROUNDS:], source[:, SCALAR_ROUNDS:], 1.0, 0.0, MULT, ADD)
        wq_near = quantise_tiles(g1, 0, 2, "qa0", "qa0")

        win_e1 = keep.tile([P, S], F32, name="win_e1", tag="w1b")
        nc.scalar.copy(out=win_e1[:], in_=win_e0[:])
        wins = [[win_a0, win_a1, win_a0, win_a3], [win_e0, win_e1, win_e2, win_e0]]
        lists = [near_t, far_t]

        gw = keep.tile([P, S], U32, name="gw", align_bytes=64)
        for v0, v1 in ((0, V // 2), (V // 2, V), (V, S)):
            nc.vector.tensor_copy(out=gw[:, v0:v1], in_=xw[:].bitcast(U32).indirect(offs_t[:, v0 // STRIPE : v1 // STRIPE]))

        def product(sensor, t, weights, v0, v1):
            acc = psum.tile([P, V], F32, name="acc", tag="acc")
            cols = slice(sensor * V + v0, sensor * V + v1)
            nc.tensor.matmul_mx(
                out=acc[:, : v1 - v0],
                lhsT=weights[t][0].bitcast(FP8X4),
                lhsT_scale=weights[t][1],
                rhs=gw[:, cols].bitcast(FP8X4),
                rhs_scale=gs[:, cols],
                start=True,
                stop=True,
            )
            return acc

        def relu_scalar(values, acc):
            nc.scalar.activation(out=values, in_=acc, func=RELU)

        def relu_vector(values, acc):
            nc.vector.tensor_scalar_max(values, acc, 0.0)

        def scatter_vector(sensor, t, v0, v1, values):
            nc.vector.tensor_copy(out=wins[sensor][t][:].indirect(lists[sensor][:, v0 // STRIPE : v1 // STRIPE]), in_=values)

        def scatter_scalar(sensor, t, v0, v1, values):
            nc.scalar.activation(out=wins[sensor][t][:].indirect(lists[sensor][:, v0 // STRIPE : v1 // STRIPE]), in_=values, func=COPY)

        def join(t, target, cells):
            nc.vector.tensor_tensor(out=target, in0=wins[NEAR][t][:, cells], in1=wins[FAR][t][:, cells], op=MAX)

        first, second = slice(0, V // 2), slice(V // 2, V)
        a0 = keep.tile([P, V], F32, name="a0")
        a1 = keep.tile([P, V], F32, name="a1")
        relu_scalar(a0[:, first], product(NEAR, 0, wq_near, 0, V // 2)[:, first])
        relu_scalar(a1[:, first], product(NEAR, 1, wq_near, 0, V // 2)[:, first])
        relu_scalar(a0[:, second], product(NEAR, 0, wq_near, V // 2, V)[:, first])
        acc_a1 = product(NEAR, 1, wq_near, V // 2, V)
        wq_near = wq_near + quantise_tiles(g1, 2, PACK, "qa2", "qa0")
        acc_a3 = product(NEAR, 3, wq_near, 0, V)
        acc_a2 = product(NEAR, 2, wq_near, 0, V)
        scatter_vector(NEAR, 0, 0, V, a0[:])
        a3 = keep.tile([P, A3_FIRST], F32, name="a3")
        scatter_scalar(NEAR, 1, 0, V // 2, a1[:, first])
        relu_scalar(a1[:, second], acc_a1[:, first])
        relu_scalar(a3[:], acc_a3[:, :A3_FIRST])
        scatter_scalar(NEAR, 1, V // 2, V, a1[:, second])
        scatter_scalar(NEAR, 3, 0, A3_FIRST, a3[:])

        g2 = keep.tile([P, PACK * H], BF16, name="g2", align_bytes=64)
        round_half(g2, w2a, 0)
        round_half(g2, w2b, 1)
        wq_far = quantise_tiles(g2, 0, 1, "qe0", "qe0") + quantise_tiles(g2, 1, PACK, "qe1", "qe1")
        acc_e0 = product(FAR, 0, wq_far, 0, V)
        acc_e1 = [product(FAR, 1, wq_far, v.start, v.stop) for v in (first, second)]
        acc_e2 = product(FAR, 2, wq_far, 0, V)
        acc_e3 = product(FAR, 3, wq_far, 0, V)
        a2 = keep.tile([P, V], F32, name="a2", tag="w2b")
        e0 = keep.tile([P, V], F32, name="e0")
        e1 = [keep.tile([P, V // 2], F32, name=f"e1{h}", tag=f"e1{h}") for h in range(2)]
        e2 = keep.tile([P, E2_FIRST], F32, name="e2")
        e3 = keep.tile([P, V], F32, name="e3")
        relu_vector(a2[:, first], acc_a2[:, first])
        relu_vector(e0[:], acc_e0[:])
        relu_vector(a2[:, second], acc_a2[:, second])
        scatter_vector(FAR, 0, 0, V, e0[:])
        relu_vector(e3[:], acc_e3[:])
        relu_scalar(e1[0][:], acc_e1[0][:, first])
        relu_scalar(e1[1][:], acc_e1[1][:, first])
        scatter_scalar(FAR, 1, 0, V // 2, e1[0][:])
        relu_scalar(e2[:], acc_e2[:, :E2_FIRST])
        scatter_scalar(FAR, 1, V // 2, V, e1[1][:])

        z01 = keep.tile([P, 2, S], BF16, name="z01", tag="z01")
        woven = keep.tile([P, S * PACK], BF16, name="woven", align_bytes=64)
        zin = [woven[:, PACK * cells.start : PACK * cells.stop].rearrange("p (c t) -> p c t", t=PACK) for cells in CHUNKS]
        join(0, z01[:, 0, :], slice(0, S))
        join(1, z01[:, 1, :], slice(0, S))
        nc.gpsimd.tensor_scalar(woven[:].rearrange("p (c t) -> p c t", t=PACK)[:, :, :2], z01[:].rearrange("p t c -> p c t"), 1.0, 0.0, MULT, ADD)

        late = keep.tile([P, 2 * V - E2_FIRST - A3_FIRST], F32, name="late", tag="win_a1")
        e2_rest, a3_rest = late[:, : V - E2_FIRST], late[:, V - E2_FIRST :]
        scatter_scalar(FAR, 2, 0, E2_FIRST, e2[:])
        scatter_scalar(FAR, 3, 0, E3_FIRST, e3[:, :E3_FIRST])
        scatter_vector(NEAR, 2, 0, V, a2[:])
        scatter_vector(FAR, 3, E3_FIRST, V, e3[:, E3_FIRST:])
        relu_scalar(e2_rest, acc_e2[:, E2_FIRST:])
        relu_scalar(a3_rest, acc_a3[:, A3_FIRST:])
        scatter_scalar(FAR, 2, E2_FIRST, V, e2_rest)
        scatter_scalar(NEAR, 3, A3_FIRST, V, a3_rest)

        z23 = keep.tile([P, 2, S], BF16, name="z23", tag="z01")
        for t, cells in MAX_PIECES:
            join(t, z23[:, t - 2, cells], cells)

        def interleave(c, copy):
            copy(out=zin[c][:, :, 2:], in_=z23[:, :, CHUNKS[c]].rearrange("p t c -> p c t"))

        for c in range(SCALAR_CHUNKS):
            interleave(c, nc.scalar.copy)

        for c in CHUNK_ORDER:
            cells = CHUNKS[c]
            n = cells.stop - cells.start
            if c == CHUNK_ORDER[1]:
                interleave(SCALAR_CHUNKS, nc.vector.tensor_copy)
            zc = keep.tile([P, n], U32, name=f"zc{c}", align_bytes=64)
            zs = keep.tile([P, n], U8, name=f"zs{c}", align_bytes=64)
            nc.vector.quantize_mx(out=zc[:].bitcast(FP8X4), scales=zs[:], in_=woven[:, PACK * cells.start : PACK * cells.stop])
            acc = psum.tile([P, V], F32, name="acc", tag="acc")
            nc.tensor.matmul_mx(
                out=acc[:, :n],
                lhsT=w3w[:].bitcast(FP4X4),
                lhsT_scale=w3s[:],
                rhs=zc[:].bitcast(FP8X4),
                rhs_scale=zs[:],
                start=True,
                stop=True,
            )
            res = keep.tile([P, n], F32, name=f"res{c}")
            empty_bank = nc.vector.tensor_copy if c == CHUNK_ORDER[-1] else nc.scalar.copy
            empty_bank(out=res[:], in_=acc[:, :n])
            nc.sync.dma_start(out=out[:, cells], in_=res[:])
